import numpy as np
import ml_dtypes


def mxq(x, axis, fmt="e4m3"):
    dtype, down = {"e4m3": (ml_dtypes.float8_e4m3fn, 7), "e5m2": (ml_dtypes.float8_e5m2, 14)}[fmt]
    v = np.moveaxis(np.asarray(x, np.float32).astype(ml_dtypes.bfloat16).astype(np.float64), axis, -1)
    blocks = v.reshape(v.shape[:-1] + (-1, 32))
    amax = np.abs(blocks).max(-1, keepdims=True)
    byte = np.maximum(np.where(amax > 0, np.frexp(amax)[1] - 1 + 127, 0) - down, 1)
    scale = np.exp2(byte - 127.0)
    codes = (blocks / scale).astype(np.float32).astype(dtype).astype(np.float64)
    return np.moveaxis((codes * scale).reshape(v.shape), -1, axis)


WIDE = False


def mx_kscale(k):
    if not WIDE:
        return np.ones(k)
    levels = np.array([18, -18])
    if k % 512:
        return np.exp2(np.random.permutation(np.resize(levels, k // 32))).repeat(32)
    a = np.empty((k // 512, 16))
    for p in range(k // 512):
        a[p, :8] = np.random.permutation(np.resize(levels, 8))
        for g in range(8):
            far = levels[np.abs(levels - a[p, g]) >= 10]
            a[p, g + 8] = far[np.random.randint(len(far))]
    return np.exp2(a.ravel()).repeat(32)


def f64(x):
    return np.asarray(x).astype(np.float64)


def striped(idx):
    return np.tile(np.asarray(idx).reshape(-1, 16).T, (8, 1)).astype(np.uint16)


def unstriped(offs):
    return offs[:16].T.reshape(-1).astype(np.int64)


B, N, T, D, R = 1, 512, 2048, 512, 1024


def setup_inputs():
    n = np.random.standard_normal
    idx = np.random.permutation(T)[:B * N]
    u = np.ones(T)
    u[idx] = mx_kscale(B * N)
    us = u[idx].reshape(B, N)
    z = mx_kscale(R)[:, None]
    act = n((B, R, N))
    return {
        "zT": (act.transpose(0, 2, 1) * us[:, :, None]).astype(np.float32),
        "wT": (n((D, T)) / np.sqrt(N) / u).astype(np.float32),
        "xm": (n((B, R, D))).astype(np.float32),
        "wt": (np.random.uniform(0.5, 1.5, (B, R, 1)) / np.sqrt(R) * z).astype(np.float32),
        "zm": (act / z).astype(np.float32),
        "offs": striped(idx),
    }


def reference(zT, wT, xm, wt, zm, offs):
    idx = unstriped(offs)
    pick = lambda x: x[:, idx].reshape(x.shape[0], B, N).transpose(1, 0, 2)
    rec = mxq(f64(zT), 1, "e4m3").transpose(0, 2, 1) @ mxq(pick(f64(wT)), 2, "e4m3").transpose(0, 2, 1)
    q = rec - f64(xm)
    e = f64(wt) * q
    dw = mxq(e, 1, "e5m2").transpose(0, 2, 1) @ mxq(f64(zm), 1, "e4m3")
    gw = np.zeros((D, T))
    gw[:, idx] = dw.transpose(1, 0, 2).reshape(D, B * N)
    return gw

@@ -1,0 +1,250 @@
+from contextlib import ExitStack
+
+import concourse.mybir as mybir
+from concourse.masks import make_identity
+
+N, T, D, R = 512, 2048, 512, 1024
+FLOPS = 2 * 2 * N * D * R
+
+F32 = mybir.dt.float32
+BF16 = mybir.dt.bfloat16
+U32 = mybir.dt.uint32
+U16 = mybir.dt.uint16
+U8 = mybir.dt.uint8
+E4M3 = mybir.dt.float8_e4m3fn_x4
+E5M2 = mybir.dt.float8_e5m2_x4
+COPY = mybir.ActivationFunctionType.Copy
+SUB = mybir.AluOpType.subtract
+
+P = 128
+PACK = 4
+K_PASS = P * PACK
+BLOCKS = D // P
+PASSES = R // K_PASS
+
+
+def tile_attend_gdi_w_kernel(tc, zT, wT, xm, wt, zm, offs, out):
+    nc = tc.nc
+    with ExitStack() as ctx:
+        keep = ctx.enter_context(tc.tile_pool(name="keep", bufs=1))
+        shared = ctx.enter_context(tc.tile_pool(name="shared", bufs=1))
+        psum = ctx.enter_context(tc.psum_pool(name="psum", bufs=2))
+        banks = ctx.enter_context(tc.psum_pool(name="banks", bufs=1))
+
+        places = {"zm_bf0": 0, "target0_1": 3072, "zm_bf1": 4096,
+                  "zm_raw0": 6144, "zm_bf2": 12288, "atoms1": 13312, "err_bf0": 14336,
+                  "atoms_bf1": 16384, "atoms2": 16384, "atoms_bf2": 18432, "atoms3": 18432,
+                  "target1_0": 20480, "grad0_1": 20480,
+                  "diff2_0": 22528, "err_rows1_1": 24064, "atoms_bf3": 24576,
+                  "err_rows2_1": 25600, "grad1_1": 25600, "err_rows3_1": 26624, "grad2_1": 26624}
+        turned_bank = ["even", "odd", "even", "odd"]
+        acc_bank = ["even", "even", "odd", "even"]
+
+        def tile(name, shape, dtype):
+            if name in places:
+                return shared.tile(shape, dtype, name=name, align_bytes=64, offset=places[name])
+            return keep.tile(shape, dtype, name=name, align_bytes=64)
+
+        def tiles(name, count, shape, dtype):
+            return [tile("%s%d" % (name, k), shape, dtype) for k in range(count)]
+
+        offsets = keep.tile([P, N // 16], U16, name="offsets")
+        weights = keep.tile([P, PASSES * PACK], F32, name="weights")
+        identity = keep.tile([P, P], F32, name="identity")
+        table = tiles("table", BLOCKS, [P, T], F32)
+        result = tiles("result", BLOCKS - 1, [P, T], F32)
+        result.append(result[0])
+        zt_raw = tiles("zt_raw", PASSES, [P, PACK, K_PASS], F32)
+        zt_bf = tiles("zt_bf", PASSES, [P, PACK, P, PACK], BF16)
+        zt_codes = tiles("zt_codes", PASSES, [P, K_PASS], U32)
+        zt_scales = tiles("zt_scales", PASSES, [P, K_PASS], U8)
+        target = [tiles("target%d_" % b, PASSES, [P, PACK, P], F32) for b in range(BLOCKS)]
+        zm_pieces = [(0, 0, N), (1, 0, N // 2), (1, N // 2, N)]
+        zm_raw = [tile("zm_raw%d" % k, [P, PACK, hi - lo], F32)
+                  for k, (g, lo, hi) in enumerate(zm_pieces)]
+        zm_bf = [tile("zm_bf%d" % k, [P, hi - lo, PACK], BF16)
+                 for k, (g, lo, hi) in enumerate(zm_pieces)]
+        zm_codes = tiles("zm_codes", PASSES, [P, N], U32)
+        zm_scales = tiles("zm_scales", PASSES, [P, N], U8)
+        atoms = tiles("atoms", BLOCKS, [P, N], F32)
+        atoms_bf = tiles("atoms_bf", BLOCKS, [P, P, PACK], BF16)
+        atom_codes = tiles("atom_codes", BLOCKS, [P, P], U32)
+        atom_scales = tiles("atom_scales", BLOCKS, [P, P], U8)
+        diff = [tiles("diff%d_" % b, PASSES, [P, PACK, P], F32) for b in range(BLOCKS)]
+        err_rows = [tiles("err_rows%d_" % b, PASSES, [P, PACK, P], BF16) for b in range(BLOCKS)]
+        err_bf = tiles("err_bf", BLOCKS, [P, PASSES, P, PACK], BF16)
+        err_codes = tiles("err_codes", BLOCKS, [P, PASSES * P], U32)
+        err_scales = tiles("err_scales", BLOCKS, [P, PASSES * P], U8)
+        grad = [tiles("grad%d_" % b, 2, [P, N // 2], F32) for b in range(BLOCKS)]
+
+        def load_table(b):
+            nc.sync.dma_start(out=table[b][:], in_=wT[b * P:(b + 1) * P, :])
+
+        def load_target(b):
+            for g in range(PASSES):
+                rows = xm[0, g * K_PASS:(g + 1) * K_PASS, b * P:(b + 1) * P]
+                nc.sync.dma_start(out=target[b][g][:], in_=rows.rearrange("(p t) d -> p t d", t=PACK))
+
+        nc.sync.dma_start(offsets[:], offs)
+        load_table(0)
+        nc.scalar.dma_start(out=weights[:].rearrange("p (g t) -> p g t", t=PACK),
+                            in_=wt[0].rearrange("(g p t) o -> p g (t o)", p=P, t=PACK))
+        for g in range(PASSES):
+            nc.sync.dma_start(out=zt_raw[g][:],
+                              in_=zT[0, :, g * K_PASS:(g + 1) * K_PASS].rearrange("(p j) r -> p j r", j=PACK))
+        load_target(0)
+        for k, (g, lo, hi) in enumerate(zm_pieces):
+            nc.sync.dma_start(out=zm_raw[k][:],
+                              in_=zm[0, g * K_PASS:(g + 1) * K_PASS, lo:hi].rearrange("(p t) i -> p t i", t=PACK))
+        load_table(1)
+        for b in range(1, BLOCKS):
+            if b + 1 < BLOCKS:
+                load_table(b + 1)
+            load_target(b)
+
+        make_identity(nc, identity[:])
+        nc.vector.memset(result[0][:], 0.0)
+        nc.vector.memset(result[1][:], 0.0)
+        nc.gpsimd.memset(result[2][:], 0.0)
+
+        def gather(b):
+            nc.vector.tensor_copy(atoms[b][:], table[b][:].indirect(offsets[:]))
+
+        def turn(b):
+            turned = banks.tile([P, PACK, P], F32, name="turned%d" % b, tag=turned_bank[b])
+            for j in range(PACK):
+                nc.tensor.transpose(turned[:, j, :], atoms[b][:, j:N:PACK], identity[:])
+            nc.scalar.copy(out=atoms_bf[b][:], in_=turned[:].rearrange("p j d -> p d j"))
+
+        recs = {}
+        accs = {}
+        half = N // 2
+
+        def rebuild(b, passes):
+            if passes[0] == 0:
+                nc.vector.quantize_mx(out=atom_codes[b][:].bitcast(E4M3), scales=atom_scales[b][:],
+                                      in_=atoms_bf[b][:].rearrange("p d j -> p (d j)"))
+            for g in passes:
+                rec = psum.tile([P, PACK, P], F32, name="rec%d" % g)
+                recs[b, g] = rec
+                for t in range(PACK):
+                    cols = slice(t * P, (t + 1) * P)
+                    nc.tensor.matmul_mx(out=rec[:, t, :],
+                                        lhsT=zt_codes[g][:, cols].bitcast(E4M3), lhsT_scale=zt_scales[g][:, cols],
+                                        rhs=atom_codes[b][:].bitcast(E4M3), rhs_scale=atom_scales[b][:],
+                                        start=True, stop=True)
+
+        def cast_zt(g):
+            nc.vector.tensor_copy(out=zt_bf[g][:].rearrange("p t m j -> p m j t"),
+                                  in_=zt_raw[g][:].rearrange("p j (m t) -> p m j t", t=PACK))
+
+        def quantise_zt(g):
+            nc.vector.quantize_mx(out=zt_codes[g][:].bitcast(E4M3), scales=zt_scales[g][:],
+                                  in_=zt_bf[g][:].rearrange("p t m j -> p (t m j)"))
+
+        def cast_zm(k):
+            nc.vector.tensor_copy(out=zm_bf[k][:].rearrange("p (c i) t -> p c t i", i=PACK),
+                                  in_=zm_raw[k][:].rearrange("p t (c i) -> p c t i", i=PACK))
+
+        def quantise_zm(k):
+            g, lo, hi = zm_pieces[k]
+            nc.vector.quantize_mx(out=zm_codes[g][:, lo:hi].bitcast(E4M3), scales=zm_scales[g][:, lo:hi],
+                                  in_=zm_bf[k][:].rearrange("p i t -> p (i t)"))
+
+        def subtract(b, g):
+            nc.vector.tensor_tensor(diff[b][g][:], recs[b, g][:], target[b][g][:], SUB)
+
+        def weigh(b, g):
+            for t in range(PACK):
+                k = g * PACK + t
+                nc.scalar.activation(err_rows[b][g][:, t, :], diff[b][g][:, t, :], COPY,
+                                     scale=weights[:, k:k + 1])
+            nc.scalar.copy(out=err_bf[b][:, g, :, :].rearrange("p (c i) t -> p c t i", i=PACK),
+                           in_=err_rows[b][g][:].rearrange("p t (c i) -> p c t i", i=PACK))
+
+        def quantise_error(b):
+            nc.vector.quantize_mx(out=err_codes[b][:].bitcast(E5M2), scales=err_scales[b][:],
+                                  in_=err_bf[b][:].rearrange("p g d t -> p (g d t)"))
+
+        def gradient(b):
+            acc = banks.tile([P, N], F32, name="acc%d" % b, tag=acc_bank[b])
+            accs[b] = acc
+            for g in range(PASSES):
+                cols = slice(g * P, (g + 1) * P)
+                nc.tensor.matmul_mx(out=acc[:],
+                                    lhsT=err_codes[b][:, cols].bitcast(E5M2), lhsT_scale=err_scales[b][:, cols],
+                                    rhs=zm_codes[g][:].bitcast(E4M3), rhs_scale=zm_scales[g][:],
+                                    start=(g == 0), stop=(g == PASSES - 1))
+
+        def drain(b, h):
+            nc.scalar.copy(out=grad[b][h][:], in_=accs[b][:, h * half:(h + 1) * half])
+
+        def scatter(b, h):
+            nc.vector.tensor_copy(result[b][:].indirect(offsets[:, h * half // 16:(h + 1) * half // 16]),
+                                  grad[b][h][:])
+            if h == 1:
+                nc.sync.dma_start(out=out[b * P:(b + 1) * P, :], in_=result[b][:])
+
+        gather(0)
+        turn(0)
+        cast_zt(0)
+        quantise_zt(0)
+        rebuild(0, [0])
+        cast_zt(1)
+        subtract(0, 0)
+        weigh(0, 0)
+        quantise_zt(1)
+        rebuild(0, [1])
+        subtract(0, 1)
+        weigh(0, 1)
+        cast_zm(0)
+        cast_zm(1)
+        quantise_zm(0)
+        quantise_zm(1)
+        cast_zm(2)
+        quantise_error(0)
+        quantise_zm(2)
+        gradient(0)
+        drain(0, 0)
+        gather(1)
+        turn(1)
+        scatter(0, 0)
+        rebuild(1, [0, 1])
+        gather(2)
+        subtract(1, 0)
+        drain(0, 1)
+        weigh(1, 0)
+        turn(2)
+        subtract(1, 1)
+        weigh(1, 1)
+        scatter(0, 1)
+        rebuild(2, [0, 1])
+        gather(3)
+        turn(3)
+        quantise_error(1)
+        gradient(1)
+        drain(1, 0)
+        subtract(2, 0)
+        weigh(2, 0)
+        subtract(2, 1)
+        weigh(2, 1)
+        rebuild(3, [0, 1])
+        scatter(1, 0)
+        subtract(3, 0)
+        subtract(3, 1)
+        quantise_error(2)
+        drain(1, 1)
+        gradient(2)
+        drain(2, 0)
+        weigh(3, 0)
+        weigh(3, 1)
+        scatter(1, 1)
+        scatter(2, 0)
+        quantise_error(3)
+        drain(2, 1)
+        gradient(3)
+        drain(3, 0)
+        drain(3, 1)
+        scatter(2, 1)
+        scatter(3, 0)
+        scatter(3, 1)

@@ -21,6 +21,29 @@ PACK = 4
 K_PASS = P * PACK
 BLOCKS = D // P
 PASSES = R // K_PASS
+HALF = N // 2
+
+PLACES = {
+    "zt_raw": 0, "diff0_0": 0, "diff0_1": 0, "diff1_0": 4096, "diff1_1": 3072,
+    "atoms_bf2": 5632, "err_codes0": 5120, "atoms3": 6144,
+    "atoms_bf1": 16384, "zt_bf0": 16384,
+    "atoms1": 20480, "zt_bf1": 20480, "atoms2": 20480,
+    "err_rows0_1": 24576, "zm_bf0_0": 24576,
+    "zm_raw0_0": 26624, "zm_bf1_0": 26624, "atoms_bf3": 28672, "zm_bf1_1": 26624,
+    "diff2_0": 30720, "zm_bf0_1": 30720,
+    "zm_raw0_1": 32768, "grad0_0": 32768, "grad1_0": 33792, "err_rows2_1": 34816,
+    "err_rows3_1": 37376, "grad1_1": 36864, "grad2": 37888,
+}
+BANKS = {
+    "turned0": 0, "turned2": 0, "acc0": 0,
+    "turned1": 1, "turned3": 1, "acc1": 1,
+    "rec0_0": 2, "rec2_0": 2, "acc2": 2,
+    "rec1_0": 3, "rec2_1": 3, "acc3": 3,
+    "rec0_1": 4, "rec3_0": 4,
+    "rec1_1": 5, "rec3_1": 5,
+    "early0": 6,
+    "early1": 7,
+}
 
 
 def tile_attend_gdi_w_kernel(tc, zT, wT, xm, wt, zm, offs, out):
@@ -28,25 +51,18 @@ def tile_attend_gdi_w_kernel(tc, zT, wT, xm, wt, zm, offs, out):
     with ExitStack() as ctx:
         keep = ctx.enter_context(tc.tile_pool(name="keep", bufs=1))
         shared = ctx.enter_context(tc.tile_pool(name="shared", bufs=1))
-        psum = ctx.enter_context(tc.psum_pool(name="psum", bufs=2))
-        banks = ctx.enter_context(tc.psum_pool(name="banks", bufs=1))
-
-        places = {"zm_bf0": 0, "target0_1": 3072, "zm_bf1": 4096,
-                  "zm_raw0": 6144, "zm_bf2": 12288, "atoms1": 13312, "err_bf0": 14336,
-                  "atoms_bf1": 16384, "atoms2": 16384, "atoms_bf2": 18432, "atoms3": 18432,
-                  "target1_0": 20480, "grad0_1": 20480,
-                  "diff2_0": 22528, "err_rows1_1": 24064, "atoms_bf3": 24576,
-                  "err_rows2_1": 25600, "grad1_1": 25600, "err_rows3_1": 26624, "grad2_1": 26624}
-        turned_bank = ["even", "odd", "even", "odd"]
-        acc_bank = ["even", "even", "odd", "even"]
+        psum = ctx.enter_context(tc.psum_pool(name="psum", bufs=1))
 
         def tile(name, shape, dtype):
-            if name in places:
-                return shared.tile(shape, dtype, name=name, align_bytes=64, offset=places[name])
+            if name in PLACES:
+                return shared.tile(shape, dtype, name=name, align_bytes=64, offset=PLACES[name])
             return keep.tile(shape, dtype, name=name, align_bytes=64)
 
         def tiles(name, count, shape, dtype):
             return [tile("%s%d" % (name, k), shape, dtype) for k in range(count)]
+
+        def bank(name, shape):
+            return psum.tile(shape, F32, name=name, tag="bank%d" % BANKS[name])
 
         offsets = keep.tile([P, N // 16], U16, name="offsets")
         weights = keep.tile([P, PASSES * PACK], F32, name="weights")
@@ -54,18 +70,15 @@ def tile_attend_gdi_w_kernel(tc, zT, wT, xm, wt, zm, offs, out):
         table = tiles("table", BLOCKS, [P, T], F32)
         result = tiles("result", BLOCKS - 1, [P, T], F32)
         result.append(result[0])
-        zt_raw = tiles("zt_raw", PASSES, [P, PACK, K_PASS], F32)
+        zt_raw = tile("zt_raw", [P, PACK, R], F32)
         zt_bf = tiles("zt_bf", PASSES, [P, PACK, P, PACK], BF16)
         zt_codes = tiles("zt_codes", PASSES, [P, K_PASS], U32)
         zt_scales = tiles("zt_scales", PASSES, [P, K_PASS], U8)
-        target = [tiles("target%d_" % b, PASSES, [P, PACK, P], F32) for b in range(BLOCKS)]
-        zm_pieces = [(0, 0, N), (1, 0, N // 2), (1, N // 2, N)]
-        zm_raw = [tile("zm_raw%d" % k, [P, PACK, hi - lo], F32)
-                  for k, (g, lo, hi) in enumerate(zm_pieces)]
-        zm_bf = [tile("zm_bf%d" % k, [P, hi - lo, PACK], BF16)
-                 for k, (g, lo, hi) in enumerate(zm_pieces)]
-        zm_codes = tiles("zm_codes", PASSES, [P, N], U32)
-        zm_scales = tiles("zm_scales", PASSES, [P, N], U8)
+        target = tiles("target", PASSES, [P, PACK, D], F32)
+        zm_raw = [tiles("zm_raw%d_" % g, 2, [P, PACK, HALF], F32) for g in range(PASSES)]
+        zm_bf = [tiles("zm_bf%d_" % g, 2, [P, HALF, PACK], BF16) for g in range(PASSES)]
+        zm_codes = tiles("zm_codes", PASSES, [P, HALF + N], U32)
+        zm_scales = tiles("zm_scales", PASSES, [P, HALF + N], U8)
         atoms = tiles("atoms", BLOCKS, [P, N], F32)
         atoms_bf = tiles("atoms_bf", BLOCKS, [P, P, PACK], BF16)
         atom_codes = tiles("atom_codes", BLOCKS, [P, P], U32)
@@ -75,90 +88,99 @@ def tile_attend_gdi_w_kernel(tc, zT, wT, xm, wt, zm, offs, out):
         err_bf = tiles("err_bf", BLOCKS, [P, PASSES, P, PACK], BF16)
         err_codes = tiles("err_codes", BLOCKS, [P, PASSES * P], U32)
         err_scales = tiles("err_scales", BLOCKS, [P, PASSES * P], U8)
-        grad = [tiles("grad%d_" % b, 2, [P, N // 2], F32) for b in range(BLOCKS)]
+        grad = {(b, h * HALF): tile("grad%d_%d" % (b, h), [P, HALF], F32) for b in range(2) for h in range(2)}
+        grad.update({(b, 0): tile("grad%d" % b, [P, N], F32) for b in range(2, BLOCKS)})
+        banks = {}
 
         def load_table(b):
             nc.sync.dma_start(out=table[b][:], in_=wT[b * P:(b + 1) * P, :])
 
-        def load_target(b):
-            for g in range(PASSES):
-                rows = xm[0, g * K_PASS:(g + 1) * K_PASS, b * P:(b + 1) * P]
-                nc.sync.dma_start(out=target[b][g][:], in_=rows.rearrange("(p t) d -> p t d", t=PACK))
+        def load_target(g):
+            rows = xm[0, g * K_PASS:(g + 1) * K_PASS, :]
+            nc.sync.dma_start(out=target[g][:], in_=rows.rearrange("(p t) d -> p t d", t=PACK))
+
+        def load_zm(g, h):
+            rows = zm[0, g * K_PASS:(g + 1) * K_PASS, h * HALF:(h + 1) * HALF]
+            nc.sync.dma_start(out=zm_raw[g][h][:], in_=rows.rearrange("(p t) i -> p t i", t=PACK))
 
         nc.sync.dma_start(offsets[:], offs)
         load_table(0)
         nc.scalar.dma_start(out=weights[:].rearrange("p (g t) -> p g t", t=PACK),
                             in_=wt[0].rearrange("(g p t) o -> p g (t o)", p=P, t=PACK))
-        for g in range(PASSES):
-            nc.sync.dma_start(out=zt_raw[g][:],
-                              in_=zT[0, :, g * K_PASS:(g + 1) * K_PASS].rearrange("(p j) r -> p j r", j=PACK))
-        load_target(0)
-        for k, (g, lo, hi) in enumerate(zm_pieces):
-            nc.sync.dma_start(out=zm_raw[k][:],
-                              in_=zm[0, g * K_PASS:(g + 1) * K_PASS, lo:hi].rearrange("(p t) i -> p t i", t=PACK))
         load_table(1)
-        for b in range(1, BLOCKS):
-            if b + 1 < BLOCKS:
-                load_table(b + 1)
-            load_target(b)
+        nc.sync.dma_start(out=zt_raw[:], in_=zT[0].rearrange("(p j) r -> p j r", j=PACK))
+        load_target(0)
+        load_table(2)
+        load_target(1)
+        load_table(3)
+        for h in range(2):
+            for g in range(PASSES):
+                load_zm(g, h)
 
         make_identity(nc, identity[:])
         nc.vector.memset(result[0][:], 0.0)
         nc.vector.memset(result[1][:], 0.0)
         nc.gpsimd.memset(result[2][:], 0.0)
+        for g in range(PASSES):
+            nc.gpsimd.memset(zm_codes[g][:, 0:HALF], 0)
+            nc.gpsimd.memset(zm_scales[g][:, 0:HALF].bitcast(U32), 0)
 
         def gather(b):
             nc.vector.tensor_copy(atoms[b][:], table[b][:].indirect(offsets[:]))
-
-        def turn(b):
-            turned = banks.tile([P, PACK, P], F32, name="turned%d" % b, tag=turned_bank[b])
+            turned = bank("turned%d" % b, [P, PACK, P])
+            banks["turned", b] = turned
             for j in range(PACK):
                 nc.tensor.transpose(turned[:, j, :], atoms[b][:, j:N:PACK], identity[:])
-            nc.scalar.copy(out=atoms_bf[b][:], in_=turned[:].rearrange("p j d -> p d j"))
 
-        recs = {}
-        accs = {}
-        half = N // 2
+        def cast_atoms(b):
+            nc.scalar.copy(out=atoms_bf[b][:], in_=banks["turned", b][:].rearrange("p j d -> p d j"))
 
-        def rebuild(b, passes):
-            if passes[0] == 0:
-                nc.vector.quantize_mx(out=atom_codes[b][:].bitcast(E4M3), scales=atom_scales[b][:],
-                                      in_=atoms_bf[b][:].rearrange("p d j -> p (d j)"))
-            for g in passes:
-                rec = psum.tile([P, PACK, P], F32, name="rec%d" % g)
-                recs[b, g] = rec
-                for t in range(PACK):
-                    cols = slice(t * P, (t + 1) * P)
-                    nc.tensor.matmul_mx(out=rec[:, t, :],
-                                        lhsT=zt_codes[g][:, cols].bitcast(E4M3), lhsT_scale=zt_scales[g][:, cols],
-                                        rhs=atom_codes[b][:].bitcast(E4M3), rhs_scale=atom_scales[b][:],
-                                        start=True, stop=True)
+        def quantise_atoms(b):
+            nc.vector.quantize_mx(out=atom_codes[b][:].bitcast(E4M3), scales=atom_scales[b][:],
+                                  in_=atoms_bf[b][:].rearrange("p d j -> p (d j)"))
+
+        def rebuild(b, g):
+            rec = bank("rec%d_%d" % (b, g), [P, PACK, P])
+            banks["rec", b, g] = rec
+            for t in range(PACK):
+                cols = slice(t * P, (t + 1) * P)
+                nc.tensor.matmul_mx(out=rec[:, t, :],
+                                    lhsT=zt_codes[g][:, cols].bitcast(E4M3), lhsT_scale=zt_scales[g][:, cols],
+                                    rhs=atom_codes[b][:].bitcast(E4M3), rhs_scale=atom_scales[b][:],
+                                    start=True, stop=True)
 
         def cast_zt(g):
-            nc.vector.tensor_copy(out=zt_bf[g][:].rearrange("p t m j -> p m j t"),
-                                  in_=zt_raw[g][:].rearrange("p j (m t) -> p m j t", t=PACK))
+            cols = zt_raw[:, :, g * K_PASS:(g + 1) * K_PASS]
+            copy = nc.vector.tensor_copy if g == 0 else nc.scalar.copy
+            copy(out=zt_bf[g][:].rearrange("p t m j -> p m j t"), in_=cols.rearrange("p j (m t) -> p m j t", t=PACK))
 
         def quantise_zt(g):
             nc.vector.quantize_mx(out=zt_codes[g][:].bitcast(E4M3), scales=zt_scales[g][:],
                                   in_=zt_bf[g][:].rearrange("p t m j -> p (t m j)"))
 
-        def cast_zm(k):
-            nc.vector.tensor_copy(out=zm_bf[k][:].rearrange("p (c i) t -> p c t i", i=PACK),
-                                  in_=zm_raw[k][:].rearrange("p t (c i) -> p c t i", i=PACK))
+        def cast_zm(g, h):
+            src = zm_raw[g][h][:].rearrange("p t (c i) -> p c t i", i=PACK)
+            dst = zm_bf[g][h][:].rearrange("p (c i) t -> p c t i", i=PACK)
+            if g == 0:
+                nc.scalar.copy(out=dst, in_=src)
+            else:
+                nc.vector.tensor_copy(out=dst, in_=src)
 
-        def quantise_zm(k):
-            g, lo, hi = zm_pieces[k]
-            nc.vector.quantize_mx(out=zm_codes[g][:, lo:hi].bitcast(E4M3), scales=zm_scales[g][:, lo:hi],
-                                  in_=zm_bf[k][:].rearrange("p i t -> p (i t)"))
+        def quantise_zm(g, h):
+            cols = slice((h + 1) * HALF, (h + 2) * HALF)
+            nc.vector.quantize_mx(out=zm_codes[g][:, cols].bitcast(E4M3), scales=zm_scales[g][:, cols],
+                                  in_=zm_bf[g][h][:].rearrange("p i t -> p (i t)"))
 
         def subtract(b, g):
-            nc.vector.tensor_tensor(diff[b][g][:], recs[b, g][:], target[b][g][:], SUB)
+            nc.vector.tensor_tensor(diff[b][g][:], banks["rec", b, g][:], target[g][:, :, b * P:(b + 1) * P], SUB)
 
         def weigh(b, g):
             for t in range(PACK):
                 k = g * PACK + t
                 nc.scalar.activation(err_rows[b][g][:, t, :], diff[b][g][:, t, :], COPY,
                                      scale=weights[:, k:k + 1])
+
+        def interleave(b, g):
             nc.scalar.copy(out=err_bf[b][:, g, :, :].rearrange("p (c i) t -> p c t i", i=PACK),
                            in_=err_rows[b][g][:].rearrange("p t (c i) -> p c t i", i=PACK))
 
@@ -166,85 +188,102 @@ def tile_attend_gdi_w_kernel(tc, zT, wT, xm, wt, zm, offs, out):
             nc.vector.quantize_mx(out=err_codes[b][:].bitcast(E5M2), scales=err_scales[b][:],
                                   in_=err_bf[b][:].rearrange("p g d t -> p (g d t)"))
 
-        def gradient(b):
-            acc = banks.tile([P, N], F32, name="acc%d" % b, tag=acc_bank[b])
-            accs[b] = acc
+        def gradient(b, early):
+            acc = bank("%s%d" % ("early" if early else "acc", b), [P, N])
+            window = slice(0, N) if early else slice(HALF, HALF + N)
             for g in range(PASSES):
                 cols = slice(g * P, (g + 1) * P)
                 nc.tensor.matmul_mx(out=acc[:],
                                     lhsT=err_codes[b][:, cols].bitcast(E5M2), lhsT_scale=err_scales[b][:, cols],
-                                    rhs=zm_codes[g][:].bitcast(E4M3), rhs_scale=zm_scales[g][:],
+                                    rhs=zm_codes[g][:, window].bitcast(E4M3), rhs_scale=zm_scales[g][:, window],
                                     start=(g == 0), stop=(g == PASSES - 1))
+            banks["acc", b, early] = acc
 
-        def drain(b, h):
-            nc.scalar.copy(out=grad[b][h][:], in_=accs[b][:, h * half:(h + 1) * half])
+        def drain(b, lo, hi):
+            early = hi < N
+            cols = slice(HALF, N) if early else slice(lo, hi)
+            nc.scalar.copy(out=grad[b, lo][:], in_=banks["acc", b, early][:, cols])
 
-        def scatter(b, h):
-            nc.vector.tensor_copy(result[b][:].indirect(offsets[:, h * half // 16:(h + 1) * half // 16]),
-                                  grad[b][h][:])
-            if h == 1:
+        def scatter(b, lo, hi):
+            nc.vector.tensor_copy(result[b][:].indirect(offsets[:, lo // 16:hi // 16]), grad[b, lo][:])
+            if hi == N:
                 nc.sync.dma_start(out=out[b * P:(b + 1) * P, :], in_=result[b][:])
 
         gather(0)
-        turn(0)
+        gather(1)
+        cast_atoms(0)
+        quantise_atoms(0)
+        cast_atoms(1)
+        quantise_atoms(1)
         cast_zt(0)
-        quantise_zt(0)
-        rebuild(0, [0])
         cast_zt(1)
+        quantise_zt(0)
+        rebuild(0, 0)
+        rebuild(1, 0)
+        quantise_zt(1)
+        rebuild(0, 1)
+        rebuild(1, 1)
         subtract(0, 0)
         weigh(0, 0)
-        quantise_zt(1)
-        rebuild(0, [1])
-        subtract(0, 1)
-        weigh(0, 1)
-        cast_zm(0)
-        cast_zm(1)
-        quantise_zm(0)
-        quantise_zm(1)
-        cast_zm(2)
-        quantise_error(0)
-        quantise_zm(2)
-        gradient(0)
-        drain(0, 0)
-        gather(1)
-        turn(1)
-        scatter(0, 0)
-        rebuild(1, [0, 1])
         gather(2)
         subtract(1, 0)
-        drain(0, 1)
         weigh(1, 0)
-        turn(2)
+        interleave(0, 0)
+        cast_atoms(2)
+        interleave(1, 0)
+        subtract(0, 1)
+        weigh(0, 1)
         subtract(1, 1)
         weigh(1, 1)
-        scatter(0, 1)
-        rebuild(2, [0, 1])
+        interleave(0, 1)
+        quantise_atoms(2)
+        rebuild(2, 0)
+        rebuild(2, 1)
         gather(3)
-        turn(3)
-        quantise_error(1)
-        gradient(1)
-        drain(1, 0)
         subtract(2, 0)
-        weigh(2, 0)
+        quantise_error(0)
         subtract(2, 1)
-        weigh(2, 1)
-        rebuild(3, [0, 1])
-        scatter(1, 0)
+        cast_zm(0, 0)
+        interleave(1, 1)
+        cast_atoms(3)
+        weigh(2, 0)
+        quantise_zm(0, 0)
+        cast_zm(1, 0)
+        quantise_atoms(3)
+        quantise_zm(1, 0)
+        gradient(0, True)
+        rebuild(3, 0)
+        rebuild(3, 1)
+        quantise_error(1)
+        gradient(1, True)
+        cast_zm(0, 1)
+        cast_zm(1, 1)
         subtract(3, 0)
+        quantise_zm(0, 1)
+        quantise_zm(1, 1)
+        gradient(0, False)
+        gradient(1, False)
+        drain(0, 0, HALF)
+        interleave(2, 0)
+        drain(1, 0, HALF)
+        weigh(2, 1)
+        interleave(2, 1)
+        drain(0, HALF, N)
+        scatter(0, 0, HALF)
         subtract(3, 1)
-        quantise_error(2)
-        drain(1, 1)
-        gradient(2)
-        drain(2, 0)
         weigh(3, 0)
+        interleave(3, 0)
         weigh(3, 1)
-        scatter(1, 1)
-        scatter(2, 0)
+        interleave(3, 1)
+        scatter(1, 0, HALF)
+        quantise_error(2)
+        gradient(2, False)
+        scatter(0, HALF, N)
         quantise_error(3)
-        drain(2, 1)
-        gradient(3)
-        drain(3, 0)
-        drain(3, 1)
-        scatter(2, 1)
-        scatter(3, 0)
-        scatter(3, 1)
+        gradient(3, False)
+        drain(1, HALF, N)
+        drain(2, 0, N)
+        drain(3, 0, N)
+        scatter(1, HALF, N)
+        scatter(2, 0, N)
+        scatter(3, 0, N)

@@ -24,15 +24,19 @@ PASSES = R // K_PASS
 HALF = N // 2
 
 PLACES = {
-    "zt_raw": 0, "diff0_0": 0, "diff0_1": 0, "diff1_0": 4096, "diff1_1": 3072,
-    "atoms_bf2": 5632, "err_codes0": 5120, "atoms3": 6144,
+    "zt_raw": 0, "diff0_0": 0, "diff1_0": 2048, "diff0_1": 4096, "atoms3": 4096,
     "atoms_bf1": 16384, "zt_bf0": 16384,
     "atoms1": 20480, "zt_bf1": 20480, "atoms2": 20480,
-    "err_rows0_1": 24576, "zm_bf0_0": 24576,
-    "zm_raw0_0": 26624, "zm_bf1_0": 26624, "atoms_bf3": 28672, "zm_bf1_1": 26624,
-    "diff2_0": 30720, "zm_bf0_1": 30720,
-    "zm_raw0_1": 32768, "grad0_0": 32768, "grad1_0": 33792, "err_rows2_1": 34816,
-    "err_rows3_1": 37376, "grad1_1": 36864, "grad2": 37888,
+    "err_rows1_0": 24576, "zm_bf0_0": 24576,
+    "zm_raw0_0": 26624, "zm_bf1_0": 26624,
+    "err_rows0_1": 30720, "atoms_bf3": 30720,
+    "zm_raw1_0": 31744, "zm_bf0_1": 31744,
+    "zm_raw0_1": 35840, "grad0_0": 35840, "err_rows1_1": 39936, "zm_bf1_1": 38912,
+    "zm_raw1_1": 40960, "target_w2_0": 40960, "target_w2_1": 43008, "target_w3_0": 40960, "target_w3_1": 43008,
+    "target2_0": 45056, "grad1_0": 45056,
+    "rec_w2_1": 47104, "grad0_1": 47104,
+    "err_bf2": 49152, "err_bf3": 49152,
+    "rec_w3_1": 51200, "grad2_1": 51200,
 }
 BANKS = {
     "turned0": 0, "turned2": 0, "acc0": 0,
@@ -74,7 +78,10 @@ def tile_attend_gdi_w_kernel(tc, zT, wT, xm, wt, zm, offs, out):
         zt_bf = tiles("zt_bf", PASSES, [P, PACK, P, PACK], BF16)
         zt_codes = tiles("zt_codes", PASSES, [P, K_PASS], U32)
         zt_scales = tiles("zt_scales", PASSES, [P, K_PASS], U8)
-        target = tiles("target", PASSES, [P, PACK, D], F32)
+        target_pair = tiles("target_pair", PASSES, [P, PACK, 2 * P], F32)
+        target = {(b, g): tile("target%d_%d" % (b, g), [P, PACK, P], F32) for b in (2, 3) for g in range(PASSES)}
+        target_w = {(b, g): tile("target_w%d_%d" % (b, g), [P, PACK, P], F32) for b in (2, 3) for g in range(PASSES)}
+        rec_w = {(b, g): tile("rec_w%d_%d" % (b, g), [P, PACK, P], F32) for b in (2, 3) for g in range(PASSES)}
         zm_raw = [tiles("zm_raw%d_" % g, 2, [P, PACK, HALF], F32) for g in range(PASSES)]
         zm_bf = [tiles("zm_bf%d_" % g, 2, [P, HALF, PACK], BF16) for g in range(PASSES)]
         zm_codes = tiles("zm_codes", PASSES, [P, HALF + N], U32)
@@ -83,21 +90,21 @@ def tile_attend_gdi_w_kernel(tc, zT, wT, xm, wt, zm, offs, out):
         atoms_bf = tiles("atoms_bf", BLOCKS, [P, P, PACK], BF16)
         atom_codes = tiles("atom_codes", BLOCKS, [P, P], U32)
         atom_scales = tiles("atom_scales", BLOCKS, [P, P], U8)
-        diff = [tiles("diff%d_" % b, PASSES, [P, PACK, P], F32) for b in range(BLOCKS)]
-        err_rows = [tiles("err_rows%d_" % b, PASSES, [P, PACK, P], BF16) for b in range(BLOCKS)]
+        diff = [tiles("diff%d_" % b, PASSES, [P, PACK, P], F32) for b in range(2)]
+        err_rows = [tiles("err_rows%d_" % b, PASSES, [P, PACK, P], BF16) for b in range(2)]
         err_bf = tiles("err_bf", BLOCKS, [P, PASSES, P, PACK], BF16)
         err_codes = tiles("err_codes", BLOCKS, [P, PASSES * P], U32)
         err_scales = tiles("err_scales", BLOCKS, [P, PASSES * P], U8)
-        grad = {(b, h * HALF): tile("grad%d_%d" % (b, h), [P, HALF], F32) for b in range(2) for h in range(2)}
-        grad.update({(b, 0): tile("grad%d" % b, [P, N], F32) for b in range(2, BLOCKS)})
+        grad = {(b, h * HALF): tile("grad%d_%d" % (b, h), [P, HALF], F32) for b in range(3) for h in range(2)}
+        grad[3, 0] = tile("grad3", [P, N], F32)
         banks = {}
 
         def load_table(b):
             nc.sync.dma_start(out=table[b][:], in_=wT[b * P:(b + 1) * P, :])
 
-        def load_target(g):
-            rows = xm[0, g * K_PASS:(g + 1) * K_PASS, :]
-            nc.sync.dma_start(out=target[g][:], in_=rows.rearrange("(p t) d -> p t d", t=PACK))
+        def load_target(dst, g, lo, hi):
+            rows = xm[0, g * K_PASS:(g + 1) * K_PASS, lo:hi]
+            nc.sync.dma_start(out=dst[:], in_=rows.rearrange("(p t) d -> p t d", t=PACK))
 
         def load_zm(g, h):
             rows = zm[0, g * K_PASS:(g + 1) * K_PASS, h * HALF:(h + 1) * HALF]
@@ -109,13 +116,16 @@ def tile_attend_gdi_w_kernel(tc, zT, wT, xm, wt, zm, offs, out):
                             in_=wt[0].rearrange("(g p t) o -> p g (t o)", p=P, t=PACK))
         load_table(1)
         nc.sync.dma_start(out=zt_raw[:], in_=zT[0].rearrange("(p j) r -> p j r", j=PACK))
-        load_target(0)
+        for g in range(PASSES):
+            load_target(target_pair[g], g, 0, 2 * P)
         load_table(2)
-        load_target(1)
         load_table(3)
         for h in range(2):
             for g in range(PASSES):
                 load_zm(g, h)
+        for b in (2, 3):
+            for g in range(PASSES):
+                load_target(target[b, g], g, b * P, (b + 1) * P)
 
         make_identity(nc, identity[:])
         nc.vector.memset(result[0][:], 0.0)
@@ -161,10 +171,7 @@ def tile_attend_gdi_w_kernel(tc, zT, wT, xm, wt, zm, offs, out):
         def cast_zm(g, h):
             src = zm_raw[g][h][:].rearrange("p t (c i) -> p c t i", i=PACK)
             dst = zm_bf[g][h][:].rearrange("p (c i) t -> p c t i", i=PACK)
-            if g == 0:
-                nc.scalar.copy(out=dst, in_=src)
-            else:
-                nc.vector.tensor_copy(out=dst, in_=src)
+            nc.vector.tensor_copy(out=dst, in_=src)
 
         def quantise_zm(g, h):
             cols = slice((h + 1) * HALF, (h + 2) * HALF)
@@ -172,13 +179,28 @@ def tile_attend_gdi_w_kernel(tc, zT, wT, xm, wt, zm, offs, out):
                                   in_=zm_bf[g][h][:].rearrange("p i t -> p (i t)"))
 
         def subtract(b, g):
-            nc.vector.tensor_tensor(diff[b][g][:], banks["rec", b, g][:], target[g][:, :, b * P:(b + 1) * P], SUB)
+            nc.vector.tensor_tensor(diff[b][g][:], banks["rec", b, g][:], target_pair[g][:, :, b * P:(b + 1) * P], SUB)
 
         def weigh(b, g):
             for t in range(PACK):
                 k = g * PACK + t
                 nc.scalar.activation(err_rows[b][g][:, t, :], diff[b][g][:, t, :], COPY,
                                      scale=weights[:, k:k + 1])
+
+        def weigh_into(dst, src, g):
+            for t in range(PACK):
+                k = g * PACK + t
+                nc.scalar.activation(dst[:, t, :], src[:, t, :], COPY, scale=weights[:, k:k + 1])
+
+        def weigh_rec(b, g):
+            weigh_into(rec_w[b, g], banks["rec", b, g], g)
+
+        def weigh_target(b, g):
+            weigh_into(target_w[b, g], target[b, g], g)
+
+        def subtract_weighed(b, g):
+            nc.gpsimd.tensor_tensor(err_bf[b][:, g, :, :], rec_w[b, g][:].rearrange("p t d -> p d t"),
+                                    target_w[b, g][:].rearrange("p t d -> p d t"), SUB)
 
         def interleave(b, g):
             nc.scalar.copy(out=err_bf[b][:, g, :, :].rearrange("p (c i) t -> p c t i", i=PACK),
@@ -200,7 +222,7 @@ def tile_attend_gdi_w_kernel(tc, zT, wT, xm, wt, zm, offs, out):
             banks["acc", b, early] = acc
 
         def drain(b, lo, hi):
-            early = hi < N
+            early = hi < N and b < 2
             cols = slice(HALF, N) if early else slice(lo, hi)
             nc.scalar.copy(out=grad[b, lo][:], in_=banks["acc", b, early][:, cols])
 
@@ -225,65 +247,67 @@ def tile_attend_gdi_w_kernel(tc, zT, wT, xm, wt, zm, offs, out):
         rebuild(1, 1)
         subtract(0, 0)
         weigh(0, 0)
-        gather(2)
         subtract(1, 0)
         weigh(1, 0)
-        interleave(0, 0)
-        cast_atoms(2)
-        interleave(1, 0)
         subtract(0, 1)
         weigh(0, 1)
+        gather(2)
         subtract(1, 1)
-        weigh(1, 1)
+        gather(3)
+        interleave(0, 0)
+        interleave(1, 0)
         interleave(0, 1)
+        cast_atoms(2)
+        weigh(1, 1)
+        cast_atoms(3)
+        interleave(1, 1)
+        cast_zm(0, 0)
         quantise_atoms(2)
         rebuild(2, 0)
         rebuild(2, 1)
-        gather(3)
-        subtract(2, 0)
-        quantise_error(0)
-        subtract(2, 1)
-        cast_zm(0, 0)
-        interleave(1, 1)
-        cast_atoms(3)
-        weigh(2, 0)
         quantise_zm(0, 0)
+        quantise_error(0)
         cast_zm(1, 0)
         quantise_atoms(3)
         quantise_zm(1, 0)
         gradient(0, True)
         rebuild(3, 0)
-        rebuild(3, 1)
         quantise_error(1)
         gradient(1, True)
+        rebuild(3, 1)
         cast_zm(0, 1)
         cast_zm(1, 1)
-        subtract(3, 0)
         quantise_zm(0, 1)
         quantise_zm(1, 1)
         gradient(0, False)
         gradient(1, False)
+        weigh_rec(2, 0)
+        weigh_rec(2, 1)
         drain(0, 0, HALF)
-        interleave(2, 0)
+        weigh_target(2, 0)
+        weigh_target(2, 1)
         drain(1, 0, HALF)
-        weigh(2, 1)
-        interleave(2, 1)
+        subtract_weighed(2, 0)
+        subtract_weighed(2, 1)
         drain(0, HALF, N)
+        drain(1, HALF, N)
+        weigh_rec(3, 0)
+        weigh_rec(3, 1)
+        weigh_target(3, 0)
+        weigh_target(3, 1)
         scatter(0, 0, HALF)
-        subtract(3, 1)
-        weigh(3, 0)
-        interleave(3, 0)
-        weigh(3, 1)
-        interleave(3, 1)
         scatter(1, 0, HALF)
         quantise_error(2)
         gradient(2, False)
+        subtract_weighed(3, 0)
+        subtract_weighed(3, 1)
+        drain(2, 0, HALF)
         scatter(0, HALF, N)
+        scatter(1, HALF, N)
+        scatter(2, 0, HALF)
         quantise_error(3)
         gradient(3, False)
-        drain(1, HALF, N)
-        drain(2, 0, N)
+        drain(2, HALF, N)
         drain(3, 0, N)
-        scatter(1, HALF, N)
-        scatter(2, 0, N)
+        scatter(2, HALF, N)
         scatter(3, 0, N)

@@ -14,6 +14,7 @@ U8 = mybir.dt.uint8
 E4M3 = mybir.dt.float8_e4m3fn_x4
 E5M2 = mybir.dt.float8_e5m2_x4
 COPY = mybir.ActivationFunctionType.Copy
+MULT = mybir.AluOpType.mult
 SUB = mybir.AluOpType.subtract
 
 P = 128
@@ -22,31 +23,29 @@ K_PASS = P * PACK
 BLOCKS = D // P
 PASSES = R // K_PASS
 HALF = N // 2
+PAIR = 2 * P
+KB = 1024
 
 PLACES = {
-    "zt_raw": 0, "diff0_0": 0, "diff1_0": 2048, "diff0_1": 4096, "atoms3": 4096,
-    "atoms_bf1": 16384, "zt_bf0": 16384,
-    "atoms1": 20480, "zt_bf1": 20480, "atoms2": 20480,
-    "err_rows1_0": 24576, "zm_bf0_0": 24576,
-    "zm_raw0_0": 26624, "zm_bf1_0": 26624,
-    "err_rows0_1": 30720, "atoms_bf3": 30720,
-    "zm_raw1_0": 31744, "zm_bf0_1": 31744,
-    "zm_raw0_1": 35840, "grad0_0": 35840, "err_rows1_1": 39936, "zm_bf1_1": 38912,
-    "zm_raw1_1": 40960, "target_w2_0": 40960, "target_w2_1": 43008, "target_w3_0": 40960, "target_w3_1": 43008,
-    "target2_0": 45056, "grad1_0": 45056,
-    "rec_w2_1": 47104, "grad0_1": 47104,
-    "err_bf2": 49152, "err_bf3": 49152,
-    "rec_w3_1": 51200, "grad2_1": 51200,
+    "zt_raw0": 0, "target_w0_0_0": 0, "target_w0_0_1": 2 * KB, "zt_bf1_0": 0,
+    "atoms1": 8 * KB, "zt_bf0_1": 8 * KB,
+    "target0_0": 10 * KB, "zt_bf1_1": 10 * KB, "zm_bf0_0": 10 * KB,
+    "zt_raw1": 14 * KB, "target_w0_1_0": 14 * KB, "target_w0_1_1": 16 * KB, "zm_bf1_0": 14 * KB,
+    "err_bf1_1": 22 * KB, "atoms2": 22 * KB,
+    "table3": 38 * KB, "grad1_0": 38 * KB,
+    "grad0_0": 23 * KB, "zm_bf0_1": 24 * KB, "zm_bf1_1": 26 * KB,
+    "target_w1_0_0": 28 * KB, "target_w1_0_1": 30 * KB, "atoms3": 29 * KB + 512,
+    "target1_0": 32 * KB, "target_w1_1_0": 32 * KB, "target_w1_1_1": 34 * KB, "grad0_1": 32 * KB,
+    "err_rows1_1": 36 * KB, "grad1_1": 36 * KB,
 }
+GATE_COLS = (7 * KB + 512) // 4
 BANKS = {
-    "turned0": 0, "turned2": 0, "acc0": 0,
-    "turned1": 1, "turned3": 1, "acc1": 1,
-    "rec0_0": 2, "rec2_0": 2, "acc2": 2,
-    "rec1_0": 3, "rec2_1": 3, "acc3": 3,
-    "rec0_1": 4, "rec3_0": 4,
-    "rec1_1": 5, "rec3_1": 5,
-    "early0": 6,
-    "early1": 7,
+    "rec0_0_0": 0, "rec0_0_1": 1, "rec0_1_0": 2, "rec0_1_1": 3,
+    "rec1_0_0": 0, "rec1_0_1": 1, "rec1_1_0": 2, "rec1_1_1": 3,
+    "turned0": 4, "turned1": 4, "turned2": 4, "turned3": 4, "acc1": 4,
+    "early0": 5, "acc2": 5,
+    "early1": 6, "acc3": 6,
+    "acc0": 7,
 }
 
 
@@ -65,6 +64,9 @@ def tile_attend_gdi_w_kernel(tc, zT, wT, xm, wt, zm, offs, out):
         def tiles(name, count, shape, dtype):
             return [tile("%s%d" % (name, k), shape, dtype) for k in range(count)]
 
+        def grid(name, rows, count, shape, dtype):
+            return [tiles("%s%d_" % (name, a), count, shape, dtype) for a in range(rows)]
+
         def bank(name, shape):
             return psum.tile(shape, F32, name=name, tag="bank%d" % BANKS[name])
 
@@ -72,39 +74,42 @@ def tile_attend_gdi_w_kernel(tc, zT, wT, xm, wt, zm, offs, out):
         weights = keep.tile([P, PASSES * PACK], F32, name="weights")
         identity = keep.tile([P, P], F32, name="identity")
         table = tiles("table", BLOCKS, [P, T], F32)
-        result = tiles("result", BLOCKS - 1, [P, T], F32)
-        result.append(result[0])
-        zt_raw = tile("zt_raw", [P, PACK, R], F32)
-        zt_bf = tiles("zt_bf", PASSES, [P, PACK, P, PACK], BF16)
-        zt_codes = tiles("zt_codes", PASSES, [P, K_PASS], U32)
-        zt_scales = tiles("zt_scales", PASSES, [P, K_PASS], U8)
-        target_pair = tiles("target_pair", PASSES, [P, PACK, 2 * P], F32)
-        target = {(b, g): tile("target%d_%d" % (b, g), [P, PACK, P], F32) for b in (2, 3) for g in range(PASSES)}
-        target_w = {(b, g): tile("target_w%d_%d" % (b, g), [P, PACK, P], F32) for b in (2, 3) for g in range(PASSES)}
-        rec_w = {(b, g): tile("rec_w%d_%d" % (b, g), [P, PACK, P], F32) for b in (2, 3) for g in range(PASSES)}
-        zm_raw = [tiles("zm_raw%d_" % g, 2, [P, PACK, HALF], F32) for g in range(PASSES)]
-        zm_bf = [tiles("zm_bf%d_" % g, 2, [P, HALF, PACK], BF16) for g in range(PASSES)]
+        result = tiles("result", BLOCKS, [P, T], F32)
+        zt_raw = tiles("zt_raw", PASSES, [P, PACK, K_PASS], F32)
+        zt_bf = grid("zt_bf", PASSES, 2, [P, 2, P, PACK], BF16)
+        zt_codes = grid("zt_codes", PASSES, 2, [P, PAIR], U32)
+        zt_scales = grid("zt_scales", PASSES, 2, [P, PAIR], U8)
+        target = grid("target", 2, PASSES, [P, PACK, PAIR], F32)
+        target_w = [grid("target_w%d_" % q, PASSES, 2, [P, 2, PAIR], F32) for q in range(2)]
+        zm_raw = grid("zm_raw", PASSES, 2, [P, PACK, HALF], F32)
+        zm_bf = grid("zm_bf", PASSES, 2, [P, HALF, PACK], BF16)
         zm_codes = tiles("zm_codes", PASSES, [P, HALF + N], U32)
         zm_scales = tiles("zm_scales", PASSES, [P, HALF + N], U8)
-        atoms = tiles("atoms", BLOCKS, [P, N], F32)
-        atoms_bf = tiles("atoms_bf", BLOCKS, [P, P, PACK], BF16)
-        atom_codes = tiles("atom_codes", BLOCKS, [P, P], U32)
-        atom_scales = tiles("atom_scales", BLOCKS, [P, P], U8)
-        diff = [tiles("diff%d_" % b, PASSES, [P, PACK, P], F32) for b in range(2)]
-        err_rows = [tiles("err_rows%d_" % b, PASSES, [P, PACK, P], BF16) for b in range(2)]
-        err_bf = tiles("err_bf", BLOCKS, [P, PASSES, P, PACK], BF16)
-        err_codes = tiles("err_codes", BLOCKS, [P, PASSES * P], U32)
-        err_scales = tiles("err_scales", BLOCKS, [P, PASSES * P], U8)
-        grad = {(b, h * HALF): tile("grad%d_%d" % (b, h), [P, HALF], F32) for b in range(3) for h in range(2)}
-        grad[3, 0] = tile("grad3", [P, N], F32)
+        atoms = tiles("atoms", BLOCKS, [P, N], BF16)
+        atoms_bf = tiles("atoms_bf", 2, [P, PAIR * PACK], BF16)
+        atom_codes = tiles("atom_codes", 2, [P, PAIR], U32)
+        atom_scales = tiles("atom_scales", 2, [P, PAIR], U8)
+        err_rows = grid("err_rows", 2, PASSES, [P, PACK, PAIR], BF16)
+        err_bf = grid("err_bf", BLOCKS, PASSES, [P, P, PACK], BF16)
+        err_codes = grid("err_codes", BLOCKS, PASSES, [P, P], U32)
+        err_scales = grid("err_scales", BLOCKS, PASSES, [P, P], U8)
+        grad = {(0, 0): tile("grad0_0", [P, GATE_COLS], F32)[:, 0:HALF]}
+        for b, h in ((1, 0), (0, 1), (1, 1)):
+            grad[b, h * HALF] = tile("grad%d_%d" % (b, h), [P, HALF], F32)[:]
+        for b in (2, 3):
+            grad[b, 0] = tile("grad%d" % b, [P, N], F32)[:]
         banks = {}
 
         def load_table(b):
             nc.sync.dma_start(out=table[b][:], in_=wT[b * P:(b + 1) * P, :])
 
-        def load_target(dst, g, lo, hi):
-            rows = xm[0, g * K_PASS:(g + 1) * K_PASS, lo:hi]
-            nc.sync.dma_start(out=dst[:], in_=rows.rearrange("(p t) d -> p t d", t=PACK))
+        def load_zt(g):
+            cols = zT[0, :, g * K_PASS:(g + 1) * K_PASS]
+            nc.sync.dma_start(out=zt_raw[g][:], in_=cols.rearrange("(p j) r -> p j r", j=PACK))
+
+        def load_target(q, g):
+            rows = xm[0, g * K_PASS:(g + 1) * K_PASS, q * PAIR:(q + 1) * PAIR]
+            nc.sync.dma_start(out=target[q][g][:], in_=rows.rearrange("(p t) d -> p t d", t=PACK))
 
         def load_zm(g, h):
             rows = zm[0, g * K_PASS:(g + 1) * K_PASS, h * HALF:(h + 1) * HALF]
@@ -115,199 +120,184 @@ def tile_attend_gdi_w_kernel(tc, zT, wT, xm, wt, zm, offs, out):
         nc.scalar.dma_start(out=weights[:].rearrange("p (g t) -> p g t", t=PACK),
                             in_=wt[0].rearrange("(g p t) o -> p g (t o)", p=P, t=PACK))
         load_table(1)
-        nc.sync.dma_start(out=zt_raw[:], in_=zT[0].rearrange("(p j) r -> p j r", j=PACK))
         for g in range(PASSES):
-            load_target(target_pair[g], g, 0, 2 * P)
+            load_zt(g)
+            load_target(0, g)
+        for g in range(PASSES):
+            load_zm(g, 0)
         load_table(2)
         load_table(3)
-        for h in range(2):
-            for g in range(PASSES):
-                load_zm(g, h)
-        for b in (2, 3):
-            for g in range(PASSES):
-                load_target(target[b, g], g, b * P, (b + 1) * P)
+        for g in range(PASSES):
+            load_zm(g, 1)
+        for g in range(PASSES):
+            load_target(1, g)
 
         make_identity(nc, identity[:])
-        nc.vector.memset(result[0][:], 0.0)
-        nc.vector.memset(result[1][:], 0.0)
-        nc.gpsimd.memset(result[2][:], 0.0)
         for g in range(PASSES):
             nc.gpsimd.memset(zm_codes[g][:, 0:HALF], 0)
             nc.gpsimd.memset(zm_scales[g][:, 0:HALF].bitcast(U32), 0)
 
+        def clear(b):
+            engine = nc.vector if b < 2 else nc.gpsimd
+            engine.memset(result[b][:], 0.0)
+
         def gather(b):
             nc.vector.tensor_copy(atoms[b][:], table[b][:].indirect(offsets[:]))
-            turned = bank("turned%d" % b, [P, PACK, P])
-            banks["turned", b] = turned
-            for j in range(PACK):
-                nc.tensor.transpose(turned[:, j, :], atoms[b][:, j:N:PACK], identity[:])
+            words = atoms[b][:].bitcast(F32)
+            turned = bank("turned%d" % b, [P, 2, P])
+            for u in range(2):
+                nc.tensor.transpose(turned[:, u, :], words[:, u:HALF:2], identity[:])
+            dst = atoms_bf[b // 2][:].bitcast(F32)[:, (b % 2) * PAIR:(b % 2 + 1) * PAIR]
+            nc.scalar.copy(out=dst.rearrange("p (d u) -> p d u", u=2), in_=turned[:].rearrange("p u d -> p d u"))
 
-        def cast_atoms(b):
-            nc.scalar.copy(out=atoms_bf[b][:], in_=banks["turned", b][:].rearrange("p j d -> p d j"))
+        def quantise_atoms(q):
+            nc.vector.quantize_mx(out=atom_codes[q][:].bitcast(E4M3), scales=atom_scales[q][:], in_=atoms_bf[q][:])
 
-        def quantise_atoms(b):
-            nc.vector.quantize_mx(out=atom_codes[b][:].bitcast(E4M3), scales=atom_scales[b][:],
-                                  in_=atoms_bf[b][:].rearrange("p d j -> p (d j)"))
+        def rebuild(q, g):
+            for s in range(2):
+                rec = bank("rec%d_%d_%d" % (q, g, s), [P, 2, PAIR])
+                banks["rec", q, g, s] = rec
+                for t in range(2):
+                    cols = slice(t * P, (t + 1) * P)
+                    nc.tensor.matmul_mx(out=rec[:, t, :],
+                                        lhsT=zt_codes[g][s][:, cols].bitcast(E4M3), lhsT_scale=zt_scales[g][s][:, cols],
+                                        rhs=atom_codes[q][:].bitcast(E4M3), rhs_scale=atom_scales[q][:],
+                                        start=True, stop=True)
 
-        def rebuild(b, g):
-            rec = bank("rec%d_%d" % (b, g), [P, PACK, P])
-            banks["rec", b, g] = rec
-            for t in range(PACK):
-                cols = slice(t * P, (t + 1) * P)
-                nc.tensor.matmul_mx(out=rec[:, t, :],
-                                    lhsT=zt_codes[g][:, cols].bitcast(E4M3), lhsT_scale=zt_scales[g][:, cols],
-                                    rhs=atom_codes[b][:].bitcast(E4M3), rhs_scale=atom_scales[b][:],
-                                    start=True, stop=True)
+        def cast_zt(g, s):
+            src = zt_raw[g][:].rearrange("p j (m t) -> p m j t", t=PACK)[:, :, :, 2 * s:2 * s + 2]
+            copy = nc.vector.tensor_copy if s == 0 else nc.scalar.copy
+            copy(out=zt_bf[g][s][:].rearrange("p t m j -> p m j t"), in_=src)
 
-        def cast_zt(g):
-            cols = zt_raw[:, :, g * K_PASS:(g + 1) * K_PASS]
-            copy = nc.vector.tensor_copy if g == 0 else nc.scalar.copy
-            copy(out=zt_bf[g][:].rearrange("p t m j -> p m j t"), in_=cols.rearrange("p j (m t) -> p m j t", t=PACK))
+        def quantise_zt(g, s):
+            nc.vector.quantize_mx(out=zt_codes[g][s][:].bitcast(E4M3), scales=zt_scales[g][s][:],
+                                  in_=zt_bf[g][s][:].rearrange("p t m j -> p (t m j)"))
 
-        def quantise_zt(g):
-            nc.vector.quantize_mx(out=zt_codes[g][:].bitcast(E4M3), scales=zt_scales[g][:],
-                                  in_=zt_bf[g][:].rearrange("p t m j -> p (t m j)"))
-
-        def cast_zm(g, h):
+        def cast_zm(g, h, copy):
             src = zm_raw[g][h][:].rearrange("p t (c i) -> p c t i", i=PACK)
             dst = zm_bf[g][h][:].rearrange("p (c i) t -> p c t i", i=PACK)
-            nc.vector.tensor_copy(out=dst, in_=src)
+            copy(out=dst, in_=src)
 
         def quantise_zm(g, h):
             cols = slice((h + 1) * HALF, (h + 2) * HALF)
             nc.vector.quantize_mx(out=zm_codes[g][:, cols].bitcast(E4M3), scales=zm_scales[g][:, cols],
                                   in_=zm_bf[g][h][:].rearrange("p i t -> p (i t)"))
 
-        def subtract(b, g):
-            nc.vector.tensor_tensor(diff[b][g][:], banks["rec", b, g][:], target_pair[g][:, :, b * P:(b + 1) * P], SUB)
+        def weight(g, t):
+            return weights[:, g * PACK + t:g * PACK + t + 1]
 
-        def weigh(b, g):
+        def weigh_target(q, g):
             for t in range(PACK):
-                k = g * PACK + t
-                nc.scalar.activation(err_rows[b][g][:, t, :], diff[b][g][:, t, :], COPY,
-                                     scale=weights[:, k:k + 1])
+                nc.scalar.activation(target_w[q][g][t // 2][:, t % 2, :], target[q][g][:, t, :], COPY,
+                                     scale=weight(g, t))
 
-        def weigh_into(dst, src, g):
+        def residual(q, g):
             for t in range(PACK):
-                k = g * PACK + t
-                nc.scalar.activation(dst[:, t, :], src[:, t, :], COPY, scale=weights[:, k:k + 1])
-
-        def weigh_rec(b, g):
-            weigh_into(rec_w[b, g], banks["rec", b, g], g)
-
-        def weigh_target(b, g):
-            weigh_into(target_w[b, g], target[b, g], g)
-
-        def subtract_weighed(b, g):
-            nc.gpsimd.tensor_tensor(err_bf[b][:, g, :, :], rec_w[b, g][:].rearrange("p t d -> p d t"),
-                                    target_w[b, g][:].rearrange("p t d -> p d t"), SUB)
+                nc.vector.scalar_tensor_tensor(err_rows[q][g][:, t, :], banks["rec", q, g, t // 2][:, t % 2, :],
+                                               weight(g, t), target_w[q][g][t // 2][:, t % 2, :], MULT, SUB)
 
         def interleave(b, g):
-            nc.scalar.copy(out=err_bf[b][:, g, :, :].rearrange("p (c i) t -> p c t i", i=PACK),
-                           in_=err_rows[b][g][:].rearrange("p t (c i) -> p c t i", i=PACK))
+            rows = err_rows[b // 2][g][:, :, (b % 2) * P:(b % 2 + 1) * P]
+            nc.scalar.copy(out=err_bf[b][g][:].rearrange("p (c i) t -> p c t i", i=PACK),
+                           in_=rows.rearrange("p t (c i) -> p c t i", i=PACK))
 
-        def quantise_error(b):
-            nc.vector.quantize_mx(out=err_codes[b][:].bitcast(E5M2), scales=err_scales[b][:],
-                                  in_=err_bf[b][:].rearrange("p g d t -> p (g d t)"))
+        def quantise_error(b, g):
+            nc.vector.quantize_mx(out=err_codes[b][g][:].bitcast(E5M2), scales=err_scales[b][g][:],
+                                  in_=err_bf[b][g][:].rearrange("p d t -> p (d t)"))
 
-        def gradient(b, early):
-            acc = bank("%s%d" % ("early" if early else "acc", b), [P, N])
+        def gradient(b, g, early):
+            if g == 0:
+                banks["acc", b, early] = bank("%s%d" % ("early" if early else "acc", b), [P, N])
             window = slice(0, N) if early else slice(HALF, HALF + N)
-            for g in range(PASSES):
-                cols = slice(g * P, (g + 1) * P)
-                nc.tensor.matmul_mx(out=acc[:],
-                                    lhsT=err_codes[b][:, cols].bitcast(E5M2), lhsT_scale=err_scales[b][:, cols],
-                                    rhs=zm_codes[g][:, window].bitcast(E4M3), rhs_scale=zm_scales[g][:, window],
-                                    start=(g == 0), stop=(g == PASSES - 1))
-            banks["acc", b, early] = acc
+            nc.tensor.matmul_mx(out=banks["acc", b, early][:],
+                                lhsT=err_codes[b][g][:].bitcast(E5M2), lhsT_scale=err_scales[b][g][:],
+                                rhs=zm_codes[g][:, window].bitcast(E4M3), rhs_scale=zm_scales[g][:, window],
+                                start=(g == 0), stop=(g == PASSES - 1))
 
         def drain(b, lo, hi):
-            early = hi < N and b < 2
+            early = hi < N
             cols = slice(HALF, N) if early else slice(lo, hi)
-            nc.scalar.copy(out=grad[b, lo][:], in_=banks["acc", b, early][:, cols])
+            nc.scalar.copy(out=grad[b, lo], in_=banks["acc", b, early][:, cols])
 
         def scatter(b, lo, hi):
-            nc.vector.tensor_copy(result[b][:].indirect(offsets[:, lo // 16:hi // 16]), grad[b, lo][:])
+            nc.vector.tensor_copy(result[b][:].indirect(offsets[:, lo // 16:hi // 16]), grad[b, lo])
             if hi == N:
                 nc.sync.dma_start(out=out[b * P:(b + 1) * P, :], in_=result[b][:])
 
+        clear(0)
+        clear(1)
         gather(0)
+        clear(2)
         gather(1)
-        cast_atoms(0)
+        clear(3)
+        cast_zt(0, 0)
+        cast_zt(0, 1)
         quantise_atoms(0)
-        cast_atoms(1)
-        quantise_atoms(1)
-        cast_zt(0)
-        cast_zt(1)
-        quantise_zt(0)
+        quantise_zt(0, 0)
+        quantise_zt(0, 1)
+        weigh_target(0, 0)
         rebuild(0, 0)
-        rebuild(1, 0)
-        quantise_zt(1)
+        residual(0, 0)
+        cast_zt(1, 0)
+        cast_zt(1, 1)
+        quantise_zt(1, 0)
+        quantise_zt(1, 1)
+        weigh_target(0, 1)
         rebuild(0, 1)
-        rebuild(1, 1)
-        subtract(0, 0)
-        weigh(0, 0)
-        subtract(1, 0)
-        weigh(1, 0)
-        subtract(0, 1)
-        weigh(0, 1)
-        gather(2)
-        subtract(1, 1)
-        gather(3)
         interleave(0, 0)
         interleave(1, 0)
+        cast_zm(0, 0, nc.vector.tensor_copy)
+        residual(0, 1)
         interleave(0, 1)
-        cast_atoms(2)
-        weigh(1, 1)
-        cast_atoms(3)
         interleave(1, 1)
-        cast_zm(0, 0)
-        quantise_atoms(2)
-        rebuild(2, 0)
-        rebuild(2, 1)
+        cast_zm(1, 0, nc.vector.tensor_copy)
         quantise_zm(0, 0)
-        quantise_error(0)
-        cast_zm(1, 0)
-        quantise_atoms(3)
+        quantise_error(0, 0)
+        gradient(0, 0, True)
+        quantise_error(1, 0)
+        gradient(1, 0, True)
         quantise_zm(1, 0)
-        gradient(0, True)
-        rebuild(3, 0)
-        quantise_error(1)
-        gradient(1, True)
-        rebuild(3, 1)
-        cast_zm(0, 1)
-        cast_zm(1, 1)
-        quantise_zm(0, 1)
-        quantise_zm(1, 1)
-        gradient(0, False)
-        gradient(1, False)
-        weigh_rec(2, 0)
-        weigh_rec(2, 1)
+        quantise_error(0, 1)
+        gradient(0, 1, True)
+        quantise_error(1, 1)
+        gradient(1, 1, True)
         drain(0, 0, HALF)
-        weigh_target(2, 0)
-        weigh_target(2, 1)
-        drain(1, 0, HALF)
-        subtract_weighed(2, 0)
-        subtract_weighed(2, 1)
-        drain(0, HALF, N)
-        drain(1, HALF, N)
-        weigh_rec(3, 0)
-        weigh_rec(3, 1)
-        weigh_target(3, 0)
-        weigh_target(3, 1)
+        gather(2)
         scatter(0, 0, HALF)
+        drain(1, 0, HALF)
+        cast_zm(0, 1, nc.scalar.copy)
+        gather(3)
         scatter(1, 0, HALF)
-        quantise_error(2)
-        gradient(2, False)
-        subtract_weighed(3, 0)
-        subtract_weighed(3, 1)
-        drain(2, 0, HALF)
+        quantise_atoms(1)
+        rebuild(1, 0)
+        rebuild(1, 1)
+        quantise_zm(0, 1)
+        cast_zm(1, 1, nc.scalar.copy)
+        weigh_target(1, 0)
+        weigh_target(1, 1)
+        residual(1, 0)
+        quantise_zm(1, 1)
+        for b in range(2):
+            for g in range(PASSES):
+                gradient(b, g, False)
+        residual(1, 1)
+        drain(0, HALF, N)
+        interleave(2, 0)
+        interleave(3, 0)
+        interleave(2, 1)
+        interleave(3, 1)
+        drain(1, HALF, N)
+        quantise_error(2, 0)
+        gradient(2, 0, False)
+        quantise_error(3, 0)
+        gradient(3, 0, False)
         scatter(0, HALF, N)
-        scatter(1, HALF, N)
-        scatter(2, 0, HALF)
-        quantise_error(3)
-        gradient(3, False)
-        drain(2, HALF, N)
+        quantise_error(2, 1)
+        gradient(2, 1, False)
+        quantise_error(3, 1)
+        gradient(3, 1, False)
+        drain(2, 0, N)
         drain(3, 0, N)
-        scatter(2, HALF, N)
+        scatter(1, HALF, N)
+        scatter(2, 0, N)
         scatter(3, 0, N)

@@ -27,22 +27,14 @@ PAIR = 2 * P
 KB = 1024
 
 PLACES = {
-    "zt_raw0": 0, "target_w0_0_0": 0, "target_w0_0_1": 2 * KB, "zt_bf1_0": 0,
-    "atoms1": 8 * KB, "zt_bf0_1": 8 * KB,
-    "target0_0": 10 * KB, "zt_bf1_1": 10 * KB, "zm_bf0_0": 10 * KB,
-    "zt_raw1": 14 * KB, "target_w0_1_0": 14 * KB, "target_w0_1_1": 16 * KB, "zm_bf1_0": 14 * KB,
-    "err_bf1_1": 22 * KB, "atoms2": 22 * KB,
-    "table3": 38 * KB, "grad1_0": 38 * KB,
-    "grad0_0": 23 * KB, "zm_bf0_1": 24 * KB, "zm_bf1_1": 26 * KB,
-    "target_w1_0_0": 28 * KB, "target_w1_0_1": 30 * KB, "atoms3": 29 * KB + 512,
-    "target1_0": 32 * KB, "target_w1_1_0": 32 * KB, "target_w1_1_1": 34 * KB, "grad0_1": 32 * KB,
-    "err_rows1_1": 36 * KB, "grad1_1": 36 * KB,
+    "target_w0_1_0": 0, "zm_bf0_0": 0,
+    "atoms_bf1": 2 * KB, "zm_raw0_1": 3 * KB, "grad1_0": 4 * KB, "zm_bf1_1": 5 * KB,
+    "target_w1_1_1": 7 * KB, "grad1_1": 7 * KB,
 }
-GATE_COLS = (7 * KB + 512) // 4
 BANKS = {
     "rec0_0_0": 0, "rec0_0_1": 1, "rec0_1_0": 2, "rec0_1_1": 3,
     "rec1_0_0": 0, "rec1_0_1": 1, "rec1_1_0": 2, "rec1_1_1": 3,
-    "turned0": 4, "turned1": 4, "turned2": 4, "turned3": 4, "acc1": 4,
+    "turned0": 4, "turned1": 4, "acc1": 4,
     "early0": 5, "acc2": 5,
     "early1": 6, "acc3": 6,
     "acc0": 7,
@@ -93,9 +85,7 @@ def tile_attend_gdi_w_kernel(tc, zT, wT, xm, wt, zm, offs, out):
         err_bf = grid("err_bf", BLOCKS, PASSES, [P, P, PACK], BF16)
         err_codes = grid("err_codes", BLOCKS, PASSES, [P, P], U32)
         err_scales = grid("err_scales", BLOCKS, PASSES, [P, P], U8)
-        grad = {(0, 0): tile("grad0_0", [P, GATE_COLS], F32)[:, 0:HALF]}
-        for b, h in ((1, 0), (0, 1), (1, 1)):
-            grad[b, h * HALF] = tile("grad%d_%d" % (b, h), [P, HALF], F32)[:]
+        grad = {(b, h * HALF): tile("grad%d_%d" % (b, h), [P, HALF], F32)[:] for b in range(2) for h in range(2)}
         for b in (2, 3):
             grad[b, 0] = tile("grad%d" % b, [P, N], F32)[:]
         banks = {}
@@ -125,8 +115,7 @@ def tile_attend_gdi_w_kernel(tc, zT, wT, xm, wt, zm, offs, out):
             load_target(0, g)
         for g in range(PASSES):
             load_zm(g, 0)
-        load_table(2)
-        load_table(3)
+            load_table(2 + g)
         for g in range(PASSES):
             load_zm(g, 1)
         for g in range(PASSES):
@@ -144,11 +133,14 @@ def tile_attend_gdi_w_kernel(tc, zT, wT, xm, wt, zm, offs, out):
         def gather(b):
             nc.vector.tensor_copy(atoms[b][:], table[b][:].indirect(offsets[:]))
             words = atoms[b][:].bitcast(F32)
-            turned = bank("turned%d" % b, [P, 2, P])
+            if b % 2 == 0:
+                banks["turned", b // 2] = bank("turned%d" % (b // 2), [P, 2, 2, P])
             for u in range(2):
-                nc.tensor.transpose(turned[:, u, :], words[:, u:HALF:2], identity[:])
-            dst = atoms_bf[b // 2][:].bitcast(F32)[:, (b % 2) * PAIR:(b % 2 + 1) * PAIR]
-            nc.scalar.copy(out=dst.rearrange("p (d u) -> p d u", u=2), in_=turned[:].rearrange("p u d -> p d u"))
+                nc.tensor.transpose(banks["turned", b // 2][:, b % 2, u, :], words[:, u:HALF:2], identity[:])
+
+        def weave_atoms(q):
+            nc.scalar.copy(out=atoms_bf[q][:].bitcast(F32).rearrange("p (b d u) -> p b d u", b=2, u=2),
+                           in_=banks["turned", q][:].rearrange("p b u d -> p b d u"))
 
         def quantise_atoms(q):
             nc.vector.quantize_mx(out=atom_codes[q][:].bitcast(E4M3), scales=atom_scales[q][:], in_=atoms_bf[q][:])
@@ -226,77 +218,66 @@ def tile_attend_gdi_w_kernel(tc, zT, wT, xm, wt, zm, offs, out):
 
         clear(0)
         clear(1)
-        gather(0)
         clear(2)
-        gather(1)
         clear(3)
-        cast_zt(0, 0)
-        cast_zt(0, 1)
+        gather(0)
+        gather(1)
+        weave_atoms(0)
         quantise_atoms(0)
-        quantise_zt(0, 0)
-        quantise_zt(0, 1)
-        weigh_target(0, 0)
-        rebuild(0, 0)
-        residual(0, 0)
-        cast_zt(1, 0)
-        cast_zt(1, 1)
-        quantise_zt(1, 0)
-        quantise_zt(1, 1)
-        weigh_target(0, 1)
-        rebuild(0, 1)
-        interleave(0, 0)
-        interleave(1, 0)
+        for g in range(PASSES):
+            cast_zt(g, 0)
+            cast_zt(g, 1)
+            quantise_zt(g, 0)
+            quantise_zt(g, 1)
+            weigh_target(0, g)
+            rebuild(0, g)
+            residual(0, g)
+        for g in range(PASSES):
+            interleave(0, g)
+            interleave(1, g)
         cast_zm(0, 0, nc.vector.tensor_copy)
-        residual(0, 1)
-        interleave(0, 1)
-        interleave(1, 1)
-        cast_zm(1, 0, nc.vector.tensor_copy)
-        quantise_zm(0, 0)
-        quantise_error(0, 0)
-        gradient(0, 0, True)
-        quantise_error(1, 0)
-        gradient(1, 0, True)
-        quantise_zm(1, 0)
-        quantise_error(0, 1)
-        gradient(0, 1, True)
-        quantise_error(1, 1)
-        gradient(1, 1, True)
+        cast_zm(1, 0, nc.scalar.copy)
+        for g in range(PASSES):
+            quantise_error(0, g)
+            quantise_error(1, g)
+            quantise_zm(g, 0)
+            gradient(0, g, True)
+            gradient(1, g, True)
+            gather(2 + g)
         drain(0, 0, HALF)
-        gather(2)
         scatter(0, 0, HALF)
-        drain(1, 0, HALF)
         cast_zm(0, 1, nc.scalar.copy)
-        gather(3)
-        scatter(1, 0, HALF)
-        quantise_atoms(1)
-        rebuild(1, 0)
-        rebuild(1, 1)
-        quantise_zm(0, 1)
+        weave_atoms(1)
+        drain(1, 0, HALF)
         cast_zm(1, 1, nc.scalar.copy)
-        weigh_target(1, 0)
-        weigh_target(1, 1)
-        residual(1, 0)
+        quantise_zm(0, 1)
+        quantise_atoms(1)
+        scatter(1, 0, HALF)
         quantise_zm(1, 1)
+        for g in range(PASSES):
+            weigh_target(1, g)
+            rebuild(1, g)
         for b in range(2):
             for g in range(PASSES):
                 gradient(b, g, False)
-        residual(1, 1)
-        drain(0, HALF, N)
+        for g in range(PASSES):
+            residual(1, g)
         interleave(2, 0)
+        drain(0, HALF, N)
         interleave(3, 0)
         interleave(2, 1)
-        interleave(3, 1)
         drain(1, HALF, N)
+        interleave(3, 1)
         quantise_error(2, 0)
         gradient(2, 0, False)
-        quantise_error(3, 0)
-        gradient(3, 0, False)
         scatter(0, HALF, N)
         quantise_error(2, 1)
         gradient(2, 1, False)
+        drain(2, 0, N)
+        quantise_error(3, 0)
+        gradient(3, 0, False)
         quantise_error(3, 1)
         gradient(3, 1, False)
-        drain(2, 0, N)
         drain(3, 0, N)
         scatter(1, HALF, N)
         scatter(2, 0, N)

@@ -67,7 +67,7 @@ def tile_attend_gdi_w_kernel(tc, zT, wT, xm, wt, zm, offs, out):
         identity = keep.tile([P, P], F32, name="identity")
         table = tiles("table", BLOCKS, [P, T], F32)
         result = tiles("result", BLOCKS, [P, T], F32)
-        zt_raw = tiles("zt_raw", PASSES, [P, PACK, K_PASS], F32)
+        zt_raw = tile("zt_raw", [P, PACK, R], F32)
         zt_bf = grid("zt_bf", PASSES, 2, [P, 2, P, PACK], BF16)
         zt_codes = grid("zt_codes", PASSES, 2, [P, PAIR], U32)
         zt_scales = grid("zt_scales", PASSES, 2, [P, PAIR], U8)
@@ -93,10 +93,6 @@ def tile_attend_gdi_w_kernel(tc, zT, wT, xm, wt, zm, offs, out):
         def load_table(b):
             nc.sync.dma_start(out=table[b][:], in_=wT[b * P:(b + 1) * P, :])
 
-        def load_zt(g):
-            cols = zT[0, :, g * K_PASS:(g + 1) * K_PASS]
-            nc.sync.dma_start(out=zt_raw[g][:], in_=cols.rearrange("(p j) r -> p j r", j=PACK))
-
         def load_target(q, g):
             rows = xm[0, g * K_PASS:(g + 1) * K_PASS, q * PAIR:(q + 1) * PAIR]
             nc.sync.dma_start(out=target[q][g][:], in_=rows.rearrange("(p t) d -> p t d", t=PACK))
@@ -110,8 +106,8 @@ def tile_attend_gdi_w_kernel(tc, zT, wT, xm, wt, zm, offs, out):
         nc.scalar.dma_start(out=weights[:].rearrange("p (g t) -> p g t", t=PACK),
                             in_=wt[0].rearrange("(g p t) o -> p g (t o)", p=P, t=PACK))
         load_table(1)
+        nc.sync.dma_start(out=zt_raw[:], in_=zT[0].rearrange("(p j) r -> p j r", j=PACK))
         for g in range(PASSES):
-            load_zt(g)
             load_target(0, g)
         for g in range(PASSES):
             load_zm(g, 0)
@@ -157,7 +153,8 @@ def tile_attend_gdi_w_kernel(tc, zT, wT, xm, wt, zm, offs, out):
                                         start=True, stop=True)
 
         def cast_zt(g, s):
-            src = zt_raw[g][:].rearrange("p j (m t) -> p m j t", t=PACK)[:, :, :, 2 * s:2 * s + 2]
+            cols = zt_raw[:, :, g * K_PASS:(g + 1) * K_PASS]
+            src = cols.rearrange("p j (m t) -> p m j t", t=PACK)[:, :, :, 2 * s:2 * s + 2]
             copy = nc.vector.tensor_copy if s == 0 else nc.scalar.copy
             copy(out=zt_bf[g][s][:].rearrange("p t m j -> p m j t"), in_=src)
 
@@ -227,8 +224,10 @@ def tile_attend_gdi_w_kernel(tc, zT, wT, xm, wt, zm, offs, out):
         for g in range(PASSES):
             cast_zt(g, 0)
             cast_zt(g, 1)
+        for g in range(PASSES):
             quantise_zt(g, 0)
             quantise_zt(g, 1)
+        for g in range(PASSES):
             weigh_target(0, g)
             rebuild(0, g)
             residual(0, g)

@@ -213,10 +213,8 @@ def tile_attend_gdi_w_kernel(tc, zT, wT, xm, wt, zm, offs, out):
             if hi == N:
                 nc.sync.dma_start(out=out[b * P:(b + 1) * P, :], in_=result[b][:])
 
-        clear(0)
-        clear(1)
-        clear(2)
-        clear(3)
+        for b in range(BLOCKS):
+            clear(b)
         gather(0)
         gather(1)
         weave_atoms(0)
@@ -244,40 +242,31 @@ def tile_attend_gdi_w_kernel(tc, zT, wT, xm, wt, zm, offs, out):
             gradient(1, g, True)
             gather(2 + g)
         drain(0, 0, HALF)
-        scatter(0, 0, HALF)
         cast_zm(0, 1, nc.scalar.copy)
         weave_atoms(1)
         drain(1, 0, HALF)
         cast_zm(1, 1, nc.scalar.copy)
-        quantise_zm(0, 1)
         quantise_atoms(1)
-        scatter(1, 0, HALF)
-        quantise_zm(1, 1)
+        for g in range(PASSES):
+            quantise_zm(g, 1)
         for g in range(PASSES):
             weigh_target(1, g)
             rebuild(1, g)
+            residual(1, g)
         for b in range(2):
             for g in range(PASSES):
                 gradient(b, g, False)
         for g in range(PASSES):
-            residual(1, g)
-        interleave(2, 0)
-        drain(0, HALF, N)
-        interleave(3, 0)
-        interleave(2, 1)
-        drain(1, HALF, N)
-        interleave(3, 1)
-        quantise_error(2, 0)
-        gradient(2, 0, False)
-        scatter(0, HALF, N)
-        quantise_error(2, 1)
-        gradient(2, 1, False)
-        drain(2, 0, N)
-        quantise_error(3, 0)
-        gradient(3, 0, False)
-        quantise_error(3, 1)
-        gradient(3, 1, False)
-        drain(3, 0, N)
-        scatter(1, HALF, N)
-        scatter(2, 0, N)
-        scatter(3, 0, N)
+            interleave(2, g)
+            drain(g, HALF, N)
+            interleave(3, g)
+        for b in (2, 3):
+            for g in range(PASSES):
+                quantise_error(b, g)
+                gradient(b, g, False)
+            drain(b, 0, N)
+        for lo in (0, HALF):
+            for b in range(2):
+                scatter(b, lo, lo + HALF)
+        for b in (2, 3):
+            scatter(b, 0, N)

@@ -101,8 +101,8 @@ def tile_attend_gdi_w_kernel(tc, zT, wT, xm, wt, zm, offs, out):
             rows = zm[0, g * K_PASS:(g + 1) * K_PASS, h * HALF:(h + 1) * HALF]
             nc.sync.dma_start(out=zm_raw[g][h][:], in_=rows.rearrange("(p t) i -> p t i", t=PACK))
 
-        nc.sync.dma_start(offsets[:], offs)
         load_table(0)
+        nc.sync.dma_start(offsets[:], offs)
         nc.scalar.dma_start(out=weights[:].rearrange("p (g t) -> p g t", t=PACK),
                             in_=wt[0].rearrange("(g p t) o -> p g (t o)", p=P, t=PACK))
         load_table(1)
@@ -210,8 +210,11 @@ def tile_attend_gdi_w_kernel(tc, zT, wT, xm, wt, zm, offs, out):
 
         def scatter(b, lo, hi):
             nc.vector.tensor_copy(result[b][:].indirect(offsets[:, lo // 16:hi // 16]), grad[b, lo])
-            if hi == N:
+            if hi == N and b < BLOCKS - 1:
                 nc.sync.dma_start(out=out[b * P:(b + 1) * P, :], in_=result[b][:])
+            elif hi == N:
+                for queue, cols in ((nc.sync, slice(0, T // 2)), (nc.scalar, slice(T // 2, T))):
+                    queue.dma_start(out=out[b * P:(b + 1) * P, cols], in_=result[b][:, cols])
 
         for b in range(BLOCKS):
             clear(b)

@@ -24,19 +24,37 @@ BLOCKS = D // P
 PASSES = R // K_PASS
 HALF = N // 2
 PAIR = 2 * P
+BANK = 512
 KB = 1024
 
-PLACES = {
-    "target_w0_1_0": 0, "zm_bf0_0": 0,
-    "atoms_bf1": 2 * KB, "zm_raw0_1": 3 * KB, "grad1_0": 4 * KB, "zm_bf1_1": 5 * KB,
-    "target_w1_1_1": 7 * KB, "grad1_1": 7 * KB,
+GROUPS = {0: 2, 2: 1, 3: 1}
+
+GUESTS = {
+    "zm_bf0_0": ("target_w0_1_0", 0),
+    "zm_bf1_0": ("target_w0_1_1", 0),
+    "atoms2": ("target_w0_1_1", KB + KB // 2),
+    "grad0_0": ("target_first", 0),
+    "grad1_0": ("target_w0_1_1", 3 * KB // 4),
+    "zm_bf0_1": ("table2", 0),
+    "zm_bf1_1": ("table2", 4 * KB),
+    "target_w1_1_0": ("zm_raw1_1", 0),
+    "atoms3": ("table2", 0),
+    "err_rows2_0": ("table3", 0),
+    "err_rows2_1": ("table3", KB),
+    "atoms_bf3": ("target1_1", 0),
+    "grad0_1": ("target1_1", KB),
+    "err_bf2_0": ("target1_1", 2 * KB),
+    "err_rows3_0": ("target1_1", 2 * KB),
+    "err_rows3_1": ("err_bf2_1", 0),
+    "grad1_1": ("target_w1_0_1", 0),
+    "grad2": ("err_bf2_1", 0),
 }
 BANKS = {
-    "rec0_0_0": 0, "rec0_0_1": 1, "rec0_1_0": 2, "rec0_1_1": 3,
-    "rec1_0_0": 0, "rec1_0_1": 1, "rec1_1_0": 2, "rec1_1_1": 3,
-    "turned0": 4, "turned1": 4, "acc1": 4,
-    "early0": 5, "acc2": 5,
-    "early1": 6, "acc3": 6,
+    "rec0_0": 0, "rec0_1": 1, "rec0_2": 2, "rec0_3": 3,
+    "rec2_0": 0, "rec2_1": 1, "rec3_0": 2, "rec3_1": 3,
+    "turned0": 4, "turned3": 4, "acc2": 4,
+    "early0": 5, "turned2": 5, "acc3": 5,
+    "early1": 6, "acc1": 6,
     "acc0": 7,
 }
 
@@ -47,55 +65,73 @@ def tile_attend_gdi_w_kernel(tc, zT, wT, xm, wt, zm, offs, out):
         keep = ctx.enter_context(tc.tile_pool(name="keep", bufs=1))
         shared = ctx.enter_context(tc.tile_pool(name="shared", bufs=1))
         psum = ctx.enter_context(tc.psum_pool(name="psum", bufs=1))
+        places = {"end": 0}
 
-        def tile(name, shape, dtype):
-            if name in PLACES:
-                return shared.tile(shape, dtype, name=name, align_bytes=64, offset=PLACES[name])
-            return keep.tile(shape, dtype, name=name, align_bytes=64)
+        def tile(name, shape, dtype, item):
+            if name in GUESTS:
+                host, first = GUESTS[name]
+                places[name] = places[host] + first
+            else:
+                size = item
+                for count in shape[1:]:
+                    size = size * count
+                places[name] = places["end"]
+                places["end"] = places["end"] + size
+            return shared.tile(shape, dtype, name=name, align_bytes=64, offset=places[name])
 
-        def tiles(name, count, shape, dtype):
-            return [tile("%s%d" % (name, k), shape, dtype) for k in range(count)]
+        def tiles(name, keys, shape, dtype, item):
+            return {k: tile("%s%d" % (name, k), shape, dtype, item) for k in keys}
 
-        def grid(name, rows, count, shape, dtype):
-            return [tiles("%s%d_" % (name, a), count, shape, dtype) for a in range(rows)]
+        def grid(name, rows, keys, shape, dtype, item):
+            return {a: tiles("%s%d_" % (name, a), keys, shape, dtype, item) for a in rows}
 
         def bank(name, shape):
             return psum.tile(shape, F32, name=name, tag="bank%d" % BANKS[name])
 
+        two = range(2)
         offsets = keep.tile([P, N // 16], U16, name="offsets")
         weights = keep.tile([P, PASSES * PACK], F32, name="weights")
         identity = keep.tile([P, P], F32, name="identity")
-        table = tiles("table", BLOCKS, [P, T], F32)
-        result = tiles("result", BLOCKS, [P, T], F32)
-        zt_raw = tile("zt_raw", [P, PACK, R], F32)
-        zt_bf = grid("zt_bf", PASSES, 2, [P, 2, P, PACK], BF16)
-        zt_codes = grid("zt_codes", PASSES, 2, [P, PAIR], U32)
-        zt_scales = grid("zt_scales", PASSES, 2, [P, PAIR], U8)
-        target = grid("target", 2, PASSES, [P, PACK, PAIR], F32)
-        target_w = [grid("target_w%d_" % q, PASSES, 2, [P, 2, PAIR], F32) for q in range(2)]
-        zm_raw = grid("zm_raw", PASSES, 2, [P, PACK, HALF], F32)
-        zm_bf = grid("zm_bf", PASSES, 2, [P, HALF, PACK], BF16)
-        zm_codes = tiles("zm_codes", PASSES, [P, HALF + N], U32)
-        zm_scales = tiles("zm_scales", PASSES, [P, HALF + N], U8)
-        atoms = tiles("atoms", BLOCKS, [P, N], BF16)
-        atoms_bf = tiles("atoms_bf", 2, [P, PAIR * PACK], BF16)
-        atom_codes = tiles("atom_codes", 2, [P, PAIR], U32)
-        atom_scales = tiles("atom_scales", 2, [P, PAIR], U8)
-        err_rows = grid("err_rows", 2, PASSES, [P, PACK, PAIR], BF16)
-        err_bf = grid("err_bf", BLOCKS, PASSES, [P, P, PACK], BF16)
-        err_codes = grid("err_codes", BLOCKS, PASSES, [P, P], U32)
-        err_scales = grid("err_scales", BLOCKS, PASSES, [P, P], U8)
-        grad = {(b, h * HALF): tile("grad%d_%d" % (b, h), [P, HALF], F32)[:] for b in range(2) for h in range(2)}
-        for b in (2, 3):
-            grad[b, 0] = tile("grad%d" % b, [P, N], F32)[:]
+        table = tiles("table", range(BLOCKS), [P, T], F32, 4)
+        result = tiles("result", range(BLOCKS), [P, T], F32, 4)
+        zt_raw = tiles("zt_raw", two, [P, PACK, K_PASS], F32, 4)
+        zt_bf = grid("zt_bf", two, two, [P, 2, P, PACK], BF16, 2)
+        zt_codes = grid("zt_codes", two, two, [P, PAIR], U32, 4)
+        zt_scales = grid("zt_scales", two, two, [P, PAIR], U8, 1)
+        target = grid("target", two, two, [P, PACK, PAIR], F32, 4)
+        zm_raw = grid("zm_raw", two, two, [P, PACK, HALF], F32, 4)
+        target_first = tile("target_first", [P, PAIR], F32, 4)
+        target_w = {pair: grid("target_w%d_" % pair, two, two, [P, 2, PAIR], F32, 4) for pair in (1, 0)}
+        err_bf = {(b, g): tile("err_bf%d_%d" % (b, g), [P, P, PACK], BF16, 2)
+                  for b, g in [(1, 1), (1, 0), (0, 0), (2, 0), (2, 1), (0, 1), (3, 0), (3, 1)]}
+        zm_bf = grid("zm_bf", two, two, [P, HALF, PACK], BF16, 2)
+        zm_codes = tiles("zm_codes", two, [P, HALF + N], U32, 4)
+        zm_scales = tiles("zm_scales", two, [P, HALF + N], U8, 1)
+        err_rows = {q: tiles("err_rows%d_" % q, two, [P, PACK, n * P], BF16, 2) for q, n in GROUPS.items()}
+        grad = grid("grad", two, two, [P, HALF], F32, 4)
+        grad_whole = tiles("grad", (2, 3), [P, N], F32, 4)
+        atoms = tiles("atoms", range(BLOCKS), [P, N], BF16, 2)
+        atoms_bf = {q: tile("atoms_bf%d" % q, [P, n * P * PACK], BF16, 2) for q, n in GROUPS.items()}
+        atom_codes = {q: tile("atom_codes%d" % q, [P, n * P], U32, 4) for q, n in GROUPS.items()}
+        atom_scales = {q: tile("atom_scales%d" % q, [P, n * P], U8, 1) for q, n in GROUPS.items()}
+        err_codes = grid("err_codes", range(BLOCKS), two, [P, P], U32, 4)
+        err_scales = grid("err_scales", range(BLOCKS), two, [P, P], U8, 1)
         banks = {}
+
+        def group_of(b):
+            return b if b in GROUPS else b - 1
 
         def load_table(b):
             nc.sync.dma_start(out=table[b][:], in_=wT[b * P:(b + 1) * P, :])
 
-        def load_target(q, g):
-            rows = xm[0, g * K_PASS:(g + 1) * K_PASS, q * PAIR:(q + 1) * PAIR]
-            nc.sync.dma_start(out=target[q][g][:], in_=rows.rearrange("(p t) d -> p t d", t=PACK))
+        def load_target(pair, g):
+            rows = xm[0, g * K_PASS:(g + 1) * K_PASS, pair * PAIR:(pair + 1) * PAIR]
+            rows = rows.rearrange("(p t) d -> p t d", t=PACK)
+            if (pair, g) == (1, 0):
+                nc.sync.dma_start(out=target_first[:], in_=rows[:, 0, :])
+                nc.sync.dma_start(out=target[pair][g][:, 1:, :], in_=rows[:, 1:, :])
+            else:
+                nc.sync.dma_start(out=target[pair][g][:], in_=rows)
 
         def load_zm(g, h):
             rows = zm[0, g * K_PASS:(g + 1) * K_PASS, h * HALF:(h + 1) * HALF]
@@ -106,19 +142,22 @@ def tile_attend_gdi_w_kernel(tc, zT, wT, xm, wt, zm, offs, out):
         nc.scalar.dma_start(out=weights[:].rearrange("p (g t) -> p g t", t=PACK),
                             in_=wt[0].rearrange("(g p t) o -> p g (t o)", p=P, t=PACK))
         load_table(1)
-        nc.sync.dma_start(out=zt_raw[:], in_=zT[0].rearrange("(p j) r -> p j r", j=PACK))
-        for g in range(PASSES):
+        for g in two:
+            nc.sync.dma_start(out=zt_raw[g][:],
+                              in_=zT[0, :, g * K_PASS:(g + 1) * K_PASS].rearrange("(p j) r -> p j r", j=PACK))
+        for g in two:
             load_target(0, g)
-        for g in range(PASSES):
+        for g in two:
             load_zm(g, 0)
-            load_table(2 + g)
-        for g in range(PASSES):
+        load_table(2)
+        load_target(1, 0)
+        for g in two:
             load_zm(g, 1)
-        for g in range(PASSES):
-            load_target(1, g)
+        load_table(3)
+        load_target(1, 1)
 
         make_identity(nc, identity[:])
-        for g in range(PASSES):
+        for g in two:
             nc.gpsimd.memset(zm_codes[g][:, 0:HALF], 0)
             nc.gpsimd.memset(zm_scales[g][:, 0:HALF].bitcast(U32), 0)
 
@@ -127,34 +166,37 @@ def tile_attend_gdi_w_kernel(tc, zT, wT, xm, wt, zm, offs, out):
             engine.memset(result[b][:], 0.0)
 
         def gather(b):
+            q = group_of(b)
             nc.vector.tensor_copy(atoms[b][:], table[b][:].indirect(offsets[:]))
             words = atoms[b][:].bitcast(F32)
-            if b % 2 == 0:
-                banks["turned", b // 2] = bank("turned%d" % (b // 2), [P, 2, 2, P])
-            for u in range(2):
-                nc.tensor.transpose(banks["turned", b // 2][:, b % 2, u, :], words[:, u:HALF:2], identity[:])
+            if b == q:
+                banks["turned", q] = bank("turned%d" % q, [P, GROUPS[q], 2, P])
+            for u in two:
+                nc.tensor.transpose(banks["turned", q][:, b - q, u, :], words[:, u:HALF:2], identity[:])
 
         def weave_atoms(q):
-            nc.scalar.copy(out=atoms_bf[q][:].bitcast(F32).rearrange("p (b d u) -> p b d u", b=2, u=2),
+            nc.scalar.copy(out=atoms_bf[q][:].bitcast(F32).rearrange("p (b d u) -> p b d u", b=GROUPS[q], u=2),
                            in_=banks["turned", q][:].rearrange("p b u d -> p b d u"))
 
         def quantise_atoms(q):
             nc.vector.quantize_mx(out=atom_codes[q][:].bitcast(E4M3), scales=atom_scales[q][:], in_=atoms_bf[q][:])
 
         def rebuild(q, g):
-            for s in range(2):
-                rec = bank("rec%d_%d_%d" % (q, g, s), [P, 2, PAIR])
-                banks["rec", q, g, s] = rec
-                for t in range(2):
-                    cols = slice(t * P, (t + 1) * P)
-                    nc.tensor.matmul_mx(out=rec[:, t, :],
-                                        lhsT=zt_codes[g][s][:, cols].bitcast(E4M3), lhsT_scale=zt_scales[g][s][:, cols],
-                                        rhs=atom_codes[q][:].bitcast(E4M3), rhs_scale=atom_scales[q][:],
-                                        start=True, stop=True)
+            width = GROUPS[q] * P
+            per_bank = BANK // width
+            for t in range(PACK):
+                if t % per_bank == 0:
+                    rec = bank("rec%d_%d" % (q, (g * PACK + t) // per_bank), [P, per_bank, width])
+                banks["rec", q, g, t] = rec[:, t % per_bank, :]
+                cols = slice((t % 2) * P, (t % 2 + 1) * P)
+                nc.tensor.matmul_mx(out=banks["rec", q, g, t],
+                                    lhsT=zt_codes[g][t // 2][:, cols].bitcast(E4M3),
+                                    lhsT_scale=zt_scales[g][t // 2][:, cols],
+                                    rhs=atom_codes[q][:].bitcast(E4M3), rhs_scale=atom_scales[q][:],
+                                    start=True, stop=True)
 
         def cast_zt(g, s):
-            cols = zt_raw[:, :, g * K_PASS:(g + 1) * K_PASS]
-            src = cols.rearrange("p j (m t) -> p m j t", t=PACK)[:, :, :, 2 * s:2 * s + 2]
+            src = zt_raw[g][:].rearrange("p j (m t) -> p m j t", t=PACK)[:, :, :, 2 * s:2 * s + 2]
             copy = nc.vector.tensor_copy if s == 0 else nc.scalar.copy
             copy(out=zt_bf[g][s][:].rearrange("p t m j -> p m j t"), in_=src)
 
@@ -162,9 +204,10 @@ def tile_attend_gdi_w_kernel(tc, zT, wT, xm, wt, zm, offs, out):
             nc.vector.quantize_mx(out=zt_codes[g][s][:].bitcast(E4M3), scales=zt_scales[g][s][:],
                                   in_=zt_bf[g][s][:].rearrange("p t m j -> p (t m j)"))
 
-        def cast_zm(g, h, copy):
-            src = zm_raw[g][h][:].rearrange("p t (c i) -> p c t i", i=PACK)
-            dst = zm_bf[g][h][:].rearrange("p (c i) t -> p c t i", i=PACK)
+        def cast_zm(g, h, lo=0, hi=HALF):
+            src = zm_raw[g][h][:, :, lo:hi].rearrange("p t (c i) -> p c t i", i=PACK)
+            dst = zm_bf[g][h][:, lo:hi, :].rearrange("p (c i) t -> p c t i", i=PACK)
+            copy = nc.vector.tensor_copy if h == 0 else nc.scalar.copy
             copy(out=dst, in_=src)
 
         def quantise_zm(g, h):
@@ -175,24 +218,26 @@ def tile_attend_gdi_w_kernel(tc, zT, wT, xm, wt, zm, offs, out):
         def weight(g, t):
             return weights[:, g * PACK + t:g * PACK + t + 1]
 
-        def weigh_target(q, g):
-            for t in range(PACK):
-                nc.scalar.activation(target_w[q][g][t // 2][:, t % 2, :], target[q][g][:, t, :], COPY,
-                                     scale=weight(g, t))
+        def weigh_target(pair, g, places_t=range(PACK)):
+            for t in places_t:
+                rows = target_first[:] if (pair, g, t) == (1, 0, 0) else target[pair][g][:, t, :]
+                nc.scalar.activation(target_w[pair][g][t // 2][:, t % 2, :], rows, COPY, scale=weight(g, t))
 
         def residual(q, g):
+            cols = slice((q % 2) * P, (q % 2 + GROUPS[q]) * P)
             for t in range(PACK):
-                nc.vector.scalar_tensor_tensor(err_rows[q][g][:, t, :], banks["rec", q, g, t // 2][:, t % 2, :],
-                                               weight(g, t), target_w[q][g][t // 2][:, t % 2, :], MULT, SUB)
+                nc.vector.scalar_tensor_tensor(err_rows[q][g][:, t, :], banks["rec", q, g, t],
+                                               weight(g, t), target_w[q // 2][g][t // 2][:, t % 2, cols], MULT, SUB)
 
         def interleave(b, g):
-            rows = err_rows[b // 2][g][:, :, (b % 2) * P:(b % 2 + 1) * P]
-            nc.scalar.copy(out=err_bf[b][g][:].rearrange("p (c i) t -> p c t i", i=PACK),
+            q = group_of(b)
+            rows = err_rows[q][g][:, :, (b - q) * P:(b - q + 1) * P]
+            nc.scalar.copy(out=err_bf[b, g][:].rearrange("p (c i) t -> p c t i", i=PACK),
                            in_=rows.rearrange("p t (c i) -> p c t i", i=PACK))
 
         def quantise_error(b, g):
             nc.vector.quantize_mx(out=err_codes[b][g][:].bitcast(E5M2), scales=err_scales[b][g][:],
-                                  in_=err_bf[b][g][:].rearrange("p d t -> p (d t)"))
+                                  in_=err_bf[b, g][:].rearrange("p d t -> p (d t)"))
 
         def gradient(b, g, early):
             if g == 0:
@@ -203,73 +248,94 @@ def tile_attend_gdi_w_kernel(tc, zT, wT, xm, wt, zm, offs, out):
                                 rhs=zm_codes[g][:, window].bitcast(E4M3), rhs_scale=zm_scales[g][:, window],
                                 start=(g == 0), stop=(g == PASSES - 1))
 
-        def drain(b, lo, hi):
-            early = hi < N
-            cols = slice(HALF, N) if early else slice(lo, hi)
-            nc.scalar.copy(out=grad[b, lo], in_=banks["acc", b, early][:, cols])
+        def drain(b, h):
+            cols = slice(HALF, N)
+            nc.scalar.copy(out=grad[b][h][:], in_=banks["acc", b, h == 0][:, cols])
 
-        def scatter(b, lo, hi):
-            nc.vector.tensor_copy(result[b][:].indirect(offsets[:, lo // 16:hi // 16]), grad[b, lo])
-            if hi == N and b < BLOCKS - 1:
+        def store(b):
+            if b < BLOCKS - 1:
                 nc.sync.dma_start(out=out[b * P:(b + 1) * P, :], in_=result[b][:])
-            elif hi == N:
+            else:
                 for queue, cols in ((nc.sync, slice(0, T // 2)), (nc.scalar, slice(T // 2, T))):
                     queue.dma_start(out=out[b * P:(b + 1) * P, cols], in_=result[b][:, cols])
+
+        def scatter(b, h):
+            nc.vector.tensor_copy(result[b][:].indirect(offsets[:, h * HALF // 16:(h + 1) * HALF // 16]), grad[b][h][:])
+            if h == 1:
+                store(b)
+
+        def finish(b):
+            nc.scalar.copy(out=grad_whole[b][:], in_=banks["acc", b, False][:])
+            nc.vector.tensor_copy(result[b][:].indirect(offsets[:]), grad_whole[b][:])
+            store(b)
+
+        def atoms_ready(q):
+            weave_atoms(q)
+            quantise_atoms(q)
 
         for b in range(BLOCKS):
             clear(b)
         gather(0)
         gather(1)
-        weave_atoms(0)
-        quantise_atoms(0)
-        for g in range(PASSES):
+        atoms_ready(0)
+        for g in two:
             cast_zt(g, 0)
             cast_zt(g, 1)
-        for g in range(PASSES):
             quantise_zt(g, 0)
             quantise_zt(g, 1)
-        for g in range(PASSES):
+        for g in two:
             weigh_target(0, g)
             rebuild(0, g)
             residual(0, g)
-        for g in range(PASSES):
+        for g in two:
             interleave(0, g)
             interleave(1, g)
-        cast_zm(0, 0, nc.vector.tensor_copy)
-        cast_zm(1, 0, nc.scalar.copy)
-        for g in range(PASSES):
-            quantise_error(0, g)
-            quantise_error(1, g)
+        for g in two:
+            cast_zm(g, 0)
             quantise_zm(g, 0)
-            gradient(0, g, True)
-            gradient(1, g, True)
-            gather(2 + g)
-        drain(0, 0, HALF)
-        cast_zm(0, 1, nc.scalar.copy)
-        weave_atoms(1)
-        drain(1, 0, HALF)
-        cast_zm(1, 1, nc.scalar.copy)
-        quantise_atoms(1)
-        for g in range(PASSES):
-            quantise_zm(g, 1)
-        for g in range(PASSES):
-            weigh_target(1, g)
-            rebuild(1, g)
-            residual(1, g)
-        for b in range(2):
-            for g in range(PASSES):
-                gradient(b, g, False)
-        for g in range(PASSES):
-            interleave(2, g)
-            drain(g, HALF, N)
-            interleave(3, g)
-        for b in (2, 3):
-            for g in range(PASSES):
+            for b in two:
                 quantise_error(b, g)
+                gradient(b, g, True)
+        weigh_target(1, 0, [0])
+        drain(0, 0)
+        gather(2)
+        scatter(0, 0)
+        atoms_ready(2)
+        drain(1, 0)
+        weigh_target(1, 0, [1, 2, 3])
+        rebuild(2, 0)
+        rebuild(2, 1)
+        scatter(1, 0)
+        cast_zm(0, 1, 0, P)
+        cast_zm(0, 1, P, HALF)
+        quantise_zm(0, 1)
+        cast_zm(1, 1)
+        quantise_zm(1, 1)
+        for b in two:
+            for g in two:
                 gradient(b, g, False)
-            drain(b, 0, N)
-        for lo in (0, HALF):
-            for b in range(2):
-                scatter(b, lo, lo + HALF)
+        gather(3)
+        weave_atoms(3)
+        weigh_target(1, 1)
+        for g in two:
+            residual(2, g)
+        quantise_atoms(3)
+        drain(0, 1)
+        for g in two:
+            interleave(2, g)
+            rebuild(3, g)
+        scatter(0, 1)
+        for g in two:
+            quantise_error(2, g)
+            gradient(2, g, False)
+        for g in two:
+            residual(3, g)
+        drain(1, 1)
+        for g in two:
+            interleave(3, g)
+        scatter(1, 1)
+        for g in two:
+            quantise_error(3, g)
+            gradient(3, g, False)
         for b in (2, 3):
-            scatter(b, 0, N)
+            finish(b)

@@ -46,7 +46,7 @@ GUESTS = {
     "err_bf2_0": ("target1_1", 2 * KB),
     "err_rows3_0": ("target1_1", 2 * KB),
     "err_rows3_1": ("err_bf2_1", 0),
-    "grad1_1": ("target_w1_0_1", 0),
+    "grad1_1": ("target_w1_0_0", 0),
     "grad2": ("err_bf2_1", 0),
 }
 BANKS = {
@@ -93,7 +93,8 @@ def tile_attend_gdi_w_kernel(tc, zT, wT, xm, wt, zm, offs, out):
         weights = keep.tile([P, PASSES * PACK], F32, name="weights")
         identity = keep.tile([P, P], F32, name="identity")
         table = tiles("table", range(BLOCKS), [P, T], F32, 4)
-        result = tiles("result", range(BLOCKS), [P, T], F32, 4)
+        result = tiles("result", range(BLOCKS - 1), [P, T], F32, 4)
+        result[BLOCKS - 1] = result[0]
         zt_raw = tiles("zt_raw", two, [P, PACK, K_PASS], F32, 4)
         zt_bf = grid("zt_bf", two, two, [P, 2, P, PACK], BF16, 2)
         zt_codes = grid("zt_codes", two, two, [P, PAIR], U32, 4)
@@ -162,8 +163,7 @@ def tile_attend_gdi_w_kernel(tc, zT, wT, xm, wt, zm, offs, out):
             nc.gpsimd.memset(zm_scales[g][:, 0:HALF].bitcast(U32), 0)
 
         def clear(b):
-            engine = nc.vector if b < 2 else nc.gpsimd
-            engine.memset(result[b][:], 0.0)
+            nc.vector.memset(result[b][:], 0.0)
 
         def gather(b):
             q = group_of(b)
@@ -273,7 +273,7 @@ def tile_attend_gdi_w_kernel(tc, zT, wT, xm, wt, zm, offs, out):
             weave_atoms(q)
             quantise_atoms(q)
 
-        for b in range(BLOCKS):
+        for b in range(BLOCKS - 1):
             clear(b)
         gather(0)
         gather(1)

@@ -24,38 +24,11 @@ BLOCKS = D // P
 PASSES = R // K_PASS
 HALF = N // 2
 PAIR = 2 * P
-BANK = 512
-KB = 1024
-
-GROUPS = {0: 2, 2: 1, 3: 1}
+LAST = BLOCKS - 1
 
 GUESTS = {
-    "zm_bf0_0": ("target_w0_1_0", 0),
-    "zm_bf1_0": ("target_w0_1_1", 0),
-    "atoms2": ("target_w0_1_1", KB + KB // 2),
-    "grad0_0": ("target_first", 0),
-    "grad1_0": ("target_w0_1_1", 3 * KB // 4),
-    "zm_bf0_1": ("table2", 0),
-    "zm_bf1_1": ("table2", 4 * KB),
-    "target_w1_1_0": ("zm_raw1_1", 0),
-    "atoms3": ("table2", 0),
-    "err_rows2_0": ("table3", 0),
-    "err_rows2_1": ("table3", KB),
-    "atoms_bf3": ("target1_1", 0),
-    "grad0_1": ("target1_1", KB),
-    "err_bf2_0": ("target1_1", 2 * KB),
-    "err_rows3_0": ("target1_1", 2 * KB),
-    "err_rows3_1": ("err_bf2_1", 0),
-    "grad1_1": ("target_w1_0_0", 0),
-    "grad2": ("err_bf2_1", 0),
-}
-BANKS = {
-    "rec0_0": 0, "rec0_1": 1, "rec0_2": 2, "rec0_3": 3,
-    "rec2_0": 0, "rec2_1": 1, "rec3_0": 2, "rec3_1": 3,
-    "turned0": 4, "turned3": 4, "acc2": 4,
-    "early0": 5, "turned2": 5, "acc3": 5,
-    "early1": 6, "acc1": 6,
-    "acc0": 7,
+    "grad0_0": ("table2", 0),
+    "grad1_0": ("table2", 1024),
 }
 
 
@@ -85,54 +58,44 @@ def tile_attend_gdi_w_kernel(tc, zT, wT, xm, wt, zm, offs, out):
         def grid(name, rows, keys, shape, dtype, item):
             return {a: tiles("%s%d_" % (name, a), keys, shape, dtype, item) for a in rows}
 
-        def bank(name, shape):
-            return psum.tile(shape, F32, name=name, tag="bank%d" % BANKS[name])
+        def bank(name, number, shape):
+            return psum.tile(shape, F32, name=name, tag="bank%d" % number)
 
         two = range(2)
+        four = range(BLOCKS)
         offsets = keep.tile([P, N // 16], U16, name="offsets")
         weights = keep.tile([P, PASSES * PACK], F32, name="weights")
         identity = keep.tile([P, P], F32, name="identity")
-        table = tiles("table", range(BLOCKS), [P, T], F32, 4)
-        result = tiles("result", range(BLOCKS - 1), [P, T], F32, 4)
-        result[BLOCKS - 1] = result[0]
+        doubled = keep.tile([P, PASSES, PACK, 2], F32, name="doubled")
+        table = tiles("table", four, [P, T], F32, 4)
+        result = tiles("result", four, [P, T], F32, 4)
         zt_raw = tiles("zt_raw", two, [P, PACK, K_PASS], F32, 4)
         zt_bf = grid("zt_bf", two, two, [P, 2, P, PACK], BF16, 2)
         zt_codes = grid("zt_codes", two, two, [P, PAIR], U32, 4)
         zt_scales = grid("zt_scales", two, two, [P, PAIR], U8, 1)
         target = grid("target", two, two, [P, PACK, PAIR], F32, 4)
         zm_raw = grid("zm_raw", two, two, [P, PACK, HALF], F32, 4)
-        target_first = tile("target_first", [P, PAIR], F32, 4)
-        target_w = {pair: grid("target_w%d_" % pair, two, two, [P, 2, PAIR], F32, 4) for pair in (1, 0)}
-        err_bf = {(b, g): tile("err_bf%d_%d" % (b, g), [P, P, PACK], BF16, 2)
-                  for b, g in [(1, 1), (1, 0), (0, 0), (2, 0), (2, 1), (0, 1), (3, 0), (3, 1)]}
         zm_bf = grid("zm_bf", two, two, [P, HALF, PACK], BF16, 2)
-        zm_codes = tiles("zm_codes", two, [P, HALF + N], U32, 4)
-        zm_scales = tiles("zm_scales", two, [P, HALF + N], U8, 1)
-        err_rows = {q: tiles("err_rows%d_" % q, two, [P, PACK, n * P], BF16, 2) for q, n in GROUPS.items()}
-        grad = grid("grad", two, two, [P, HALF], F32, 4)
-        grad_whole = tiles("grad", (2, 3), [P, N], F32, 4)
-        atoms = tiles("atoms", range(BLOCKS), [P, N], BF16, 2)
-        atoms_bf = {q: tile("atoms_bf%d" % q, [P, n * P * PACK], BF16, 2) for q, n in GROUPS.items()}
-        atom_codes = {q: tile("atom_codes%d" % q, [P, n * P], U32, 4) for q, n in GROUPS.items()}
-        atom_scales = {q: tile("atom_scales%d" % q, [P, n * P], U8, 1) for q, n in GROUPS.items()}
-        err_codes = grid("err_codes", range(BLOCKS), two, [P, P], U32, 4)
-        err_scales = grid("err_scales", range(BLOCKS), two, [P, P], U8, 1)
+        zm_codes = tiles("zm_codes", two, [P, N], U32, 4)
+        zm_scales = tiles("zm_scales", two, [P, N], U8, 1)
+        atoms = tiles("atoms", four, [P, N], BF16, 2)
+        atoms_bf = tiles("atoms_bf", four, [P, P * PACK], BF16, 2)
+        atom_codes = tiles("atom_codes", four, [P, P], U32, 4)
+        atom_scales = tiles("atom_scales", four, [P, P], U8, 1)
+        diff = grid("diff", four, two, [P, PACK, P], F32, 4)
+        err_bf = grid("err_bf", four, two, [P, P, PACK], BF16, 2)
+        err_codes = grid("err_codes", four, two, [P, P], U32, 4)
+        err_scales = grid("err_scales", four, two, [P, P], U8, 1)
+        grad = grid("grad", four, two, [P, HALF], F32, 4)
+        grad_last = tile("grad_last", [P, N], F32, 4)
         banks = {}
-
-        def group_of(b):
-            return b if b in GROUPS else b - 1
 
         def load_table(b):
             nc.sync.dma_start(out=table[b][:], in_=wT[b * P:(b + 1) * P, :])
 
         def load_target(pair, g):
             rows = xm[0, g * K_PASS:(g + 1) * K_PASS, pair * PAIR:(pair + 1) * PAIR]
-            rows = rows.rearrange("(p t) d -> p t d", t=PACK)
-            if (pair, g) == (1, 0):
-                nc.sync.dma_start(out=target_first[:], in_=rows[:, 0, :])
-                nc.sync.dma_start(out=target[pair][g][:, 1:, :], in_=rows[:, 1:, :])
-            else:
-                nc.sync.dma_start(out=target[pair][g][:], in_=rows)
+            nc.sync.dma_start(out=target[pair][g][:], in_=rows.rearrange("(p t) d -> p t d", t=PACK))
 
         def load_zm(g, h):
             rows = zm[0, g * K_PASS:(g + 1) * K_PASS, h * HALF:(h + 1) * HALF]
@@ -151,48 +114,48 @@ def tile_attend_gdi_w_kernel(tc, zT, wT, xm, wt, zm, offs, out):
         for g in two:
             load_zm(g, 0)
         load_table(2)
-        load_target(1, 0)
         for g in two:
             load_zm(g, 1)
         load_table(3)
-        load_target(1, 1)
+        for g in two:
+            load_target(1, g)
 
         make_identity(nc, identity[:])
-        for g in two:
-            nc.gpsimd.memset(zm_codes[g][:, 0:HALF], 0)
-            nc.gpsimd.memset(zm_scales[g][:, 0:HALF].bitcast(U32), 0)
-
-        def clear(b):
+        nc.gpsimd.memset(result[LAST][:], 0.0)
+        for b in range(LAST):
             nc.vector.memset(result[b][:], 0.0)
 
+        nc.scalar.copy(out=doubled[:], in_=weights[:].rearrange("p (g t i) -> p g t i", g=PASSES, i=1)
+                       .to_broadcast([P, PASSES, PACK, 2]))
+
         def gather(b):
-            q = group_of(b)
-            nc.vector.tensor_copy(atoms[b][:], table[b][:].indirect(offsets[:]))
+            picked = table[b][:].indirect(offsets[:])
+            if b < LAST:
+                nc.scalar.activation(atoms[b][:], picked, COPY)
+            else:
+                nc.vector.tensor_copy(atoms[b][:], picked)
             words = atoms[b][:].bitcast(F32)
-            if b == q:
-                banks["turned", q] = bank("turned%d" % q, [P, GROUPS[q], 2, P])
+            banks["turned", b] = bank("turned%d" % b, 4 + b % 2, [P, 2, P])
             for u in two:
-                nc.tensor.transpose(banks["turned", q][:, b - q, u, :], words[:, u:HALF:2], identity[:])
+                nc.tensor.transpose(banks["turned", b][:, u, :], words[:, u:HALF:2], identity[:])
 
-        def weave_atoms(q):
-            nc.scalar.copy(out=atoms_bf[q][:].bitcast(F32).rearrange("p (b d u) -> p b d u", b=GROUPS[q], u=2),
-                           in_=banks["turned", q][:].rearrange("p b u d -> p b d u"))
+        def weave_atoms(b):
+            copy = nc.scalar.copy if b < 2 else nc.vector.tensor_copy
+            copy(out=atoms_bf[b][:].bitcast(F32).rearrange("p (d u) -> p d u", u=2),
+                 in_=banks["turned", b][:].rearrange("p u d -> p d u"))
 
-        def quantise_atoms(q):
-            nc.vector.quantize_mx(out=atom_codes[q][:].bitcast(E4M3), scales=atom_scales[q][:], in_=atoms_bf[q][:])
+        def quantise_atoms(b):
+            nc.vector.quantize_mx(out=atom_codes[b][:].bitcast(E4M3), scales=atom_scales[b][:], in_=atoms_bf[b][:])
 
-        def rebuild(q, g):
-            width = GROUPS[q] * P
-            per_bank = BANK // width
+        def rebuild(b, g):
+            rec = bank("rec%d_%d" % (b, g), 2 if (b, g) == (LAST, 0) else (b % 2) + 2 * g, [P, PACK, P])
+            banks["rec", b, g] = rec
             for t in range(PACK):
-                if t % per_bank == 0:
-                    rec = bank("rec%d_%d" % (q, (g * PACK + t) // per_bank), [P, per_bank, width])
-                banks["rec", q, g, t] = rec[:, t % per_bank, :]
                 cols = slice((t % 2) * P, (t % 2 + 1) * P)
-                nc.tensor.matmul_mx(out=banks["rec", q, g, t],
+                nc.tensor.matmul_mx(out=rec[:, t, :],
                                     lhsT=zt_codes[g][t // 2][:, cols].bitcast(E4M3),
                                     lhsT_scale=zt_scales[g][t // 2][:, cols],
-                                    rhs=atom_codes[q][:].bitcast(E4M3), rhs_scale=atom_scales[q][:],
+                                    rhs=atom_codes[b][:].bitcast(E4M3), rhs_scale=atom_scales[b][:],
                                     start=True, stop=True)
 
         def cast_zt(g, s):
@@ -204,138 +167,92 @@ def tile_attend_gdi_w_kernel(tc, zT, wT, xm, wt, zm, offs, out):
             nc.vector.quantize_mx(out=zt_codes[g][s][:].bitcast(E4M3), scales=zt_scales[g][s][:],
                                   in_=zt_bf[g][s][:].rearrange("p t m j -> p (t m j)"))
 
-        def cast_zm(g, h, lo=0, hi=HALF):
-            src = zm_raw[g][h][:, :, lo:hi].rearrange("p t (c i) -> p c t i", i=PACK)
-            dst = zm_bf[g][h][:, lo:hi, :].rearrange("p (c i) t -> p c t i", i=PACK)
-            copy = nc.vector.tensor_copy if h == 0 else nc.scalar.copy
+        def cast_zm(g, h):
+            src = zm_raw[g][h][:].rearrange("p t (c i) -> p c t i", i=PACK)
+            dst = zm_bf[g][h][:].rearrange("p (c i) t -> p c t i", i=PACK)
+            copy = nc.scalar.copy if h == 0 else nc.vector.tensor_copy
             copy(out=dst, in_=src)
 
         def quantise_zm(g, h):
-            cols = slice((h + 1) * HALF, (h + 2) * HALF)
+            cols = slice(h * HALF, (h + 1) * HALF)
             nc.vector.quantize_mx(out=zm_codes[g][:, cols].bitcast(E4M3), scales=zm_scales[g][:, cols],
                                   in_=zm_bf[g][h][:].rearrange("p i t -> p (i t)"))
 
-        def weight(g, t):
-            return weights[:, g * PACK + t:g * PACK + t + 1]
+        def subtract(b, g):
+            cols = slice((b % 2) * P, (b % 2 + 1) * P)
+            nc.vector.tensor_tensor(diff[b][g][:], banks["rec", b, g][:], target[b // 2][g][:, :, cols], SUB)
 
-        def weigh_target(pair, g, places_t=range(PACK)):
-            for t in places_t:
-                rows = target_first[:] if (pair, g, t) == (1, 0, 0) else target[pair][g][:, t, :]
-                nc.scalar.activation(target_w[pair][g][t // 2][:, t % 2, :], rows, COPY, scale=weight(g, t))
-
-        def residual(q, g):
-            cols = slice((q % 2) * P, (q % 2 + GROUPS[q]) * P)
-            for t in range(PACK):
-                nc.vector.scalar_tensor_tensor(err_rows[q][g][:, t, :], banks["rec", q, g, t],
-                                               weight(g, t), target_w[q // 2][g][t // 2][:, t % 2, cols], MULT, SUB)
-
-        def interleave(b, g):
-            q = group_of(b)
-            rows = err_rows[q][g][:, :, (b - q) * P:(b - q + 1) * P]
-            nc.scalar.copy(out=err_bf[b, g][:].rearrange("p (c i) t -> p c t i", i=PACK),
-                           in_=rows.rearrange("p t (c i) -> p c t i", i=PACK))
+        def weigh(b, g):
+            factor = doubled[:, g:g + 1, :, :]
+            nc.vector.tensor_tensor(err_bf[b][g][:].rearrange("p (c i) t -> p c t i", i=2),
+                                    diff[b][g][:].rearrange("p t (c i) -> p c t i", i=2),
+                                    factor.to_broadcast([P, P // 2, PACK, 2]), MULT)
 
         def quantise_error(b, g):
             nc.vector.quantize_mx(out=err_codes[b][g][:].bitcast(E5M2), scales=err_scales[b][g][:],
-                                  in_=err_bf[b, g][:].rearrange("p d t -> p (d t)"))
+                                  in_=err_bf[b][g][:].rearrange("p d t -> p (d t)"))
 
-        def gradient(b, g, early):
-            if g == 0:
-                banks["acc", b, early] = bank("%s%d" % ("early" if early else "acc", b), [P, N])
-            window = slice(0, N) if early else slice(HALF, HALF + N)
-            nc.tensor.matmul_mx(out=banks["acc", b, early][:],
-                                lhsT=err_codes[b][g][:].bitcast(E5M2), lhsT_scale=err_scales[b][g][:],
-                                rhs=zm_codes[g][:, window].bitcast(E4M3), rhs_scale=zm_scales[g][:, window],
-                                start=(g == 0), stop=(g == PASSES - 1))
-
-        def drain(b, h):
-            cols = slice(HALF, N)
-            nc.scalar.copy(out=grad[b][h][:], in_=banks["acc", b, h == 0][:, cols])
+        def gradient(key, b, cols, number):
+            acc = bank("acc%d_%d" % (b, cols.start), number, [P, cols.stop - cols.start])
+            banks["acc", key] = acc
+            order = (1, 0) if b == LAST else (0, 1)
+            for g in order:
+                nc.tensor.matmul_mx(out=acc[:],
+                                    lhsT=err_codes[b][g][:].bitcast(E5M2), lhsT_scale=err_scales[b][g][:],
+                                    rhs=zm_codes[g][:, cols].bitcast(E4M3), rhs_scale=zm_scales[g][:, cols],
+                                    start=(g == order[0]), stop=(g == order[1]))
 
         def store(b):
-            if b < BLOCKS - 1:
+            if b < LAST:
                 nc.sync.dma_start(out=out[b * P:(b + 1) * P, :], in_=result[b][:])
             else:
                 for queue, cols in ((nc.sync, slice(0, T // 2)), (nc.scalar, slice(T // 2, T))):
                     queue.dma_start(out=out[b * P:(b + 1) * P, cols], in_=result[b][:, cols])
 
-        def scatter(b, h):
-            nc.vector.tensor_copy(result[b][:].indirect(offsets[:, h * HALF // 16:(h + 1) * HALF // 16]), grad[b][h][:])
+        def half_out(b, h):
+            gradient((b, h), b, slice(h * HALF, (h + 1) * HALF), 6 + (b + h) % 2)
+            nc.scalar.copy(out=grad[b][h][:], in_=banks["acc", (b, h)][:])
+            nc.scalar.activation(result[b][:].indirect(offsets[:, h * HALF // 16:(h + 1) * HALF // 16]),
+                                 grad[b][h][:], COPY)
             if h == 1:
                 store(b)
 
-        def finish(b):
-            nc.scalar.copy(out=grad_whole[b][:], in_=banks["acc", b, False][:])
-            nc.vector.tensor_copy(result[b][:].indirect(offsets[:]), grad_whole[b][:])
-            store(b)
+        def atoms_ready(b):
+            gather(b)
+            weave_atoms(b)
+            quantise_atoms(b)
 
-        def atoms_ready(q):
-            weave_atoms(q)
-            quantise_atoms(q)
+        def errors(pair, g):
+            blocks = (2 * pair, 2 * pair + 1)
+            for step in (rebuild, subtract, weigh, quantise_error):
+                for b in blocks:
+                    step(b, g)
 
-        for b in range(BLOCKS - 1):
-            clear(b)
-        gather(0)
-        gather(1)
-        atoms_ready(0)
+        for b in two:
+            atoms_ready(b)
         for g in two:
-            cast_zt(g, 0)
-            cast_zt(g, 1)
-            quantise_zt(g, 0)
-            quantise_zt(g, 1)
+            for step in (cast_zt, quantise_zt):
+                for s in two:
+                    step(g, s)
         for g in two:
-            weigh_target(0, g)
-            rebuild(0, g)
-            residual(0, g)
-        for g in two:
-            interleave(0, g)
-            interleave(1, g)
-        for g in two:
+            errors(0, g)
             cast_zm(g, 0)
             quantise_zm(g, 0)
-            for b in two:
-                quantise_error(b, g)
-                gradient(b, g, True)
-        weigh_target(1, 0, [0])
-        drain(0, 0)
-        gather(2)
-        scatter(0, 0)
         atoms_ready(2)
-        drain(1, 0)
-        weigh_target(1, 0, [1, 2, 3])
-        rebuild(2, 0)
-        rebuild(2, 1)
-        scatter(1, 0)
-        cast_zm(0, 1, 0, P)
-        cast_zm(0, 1, P, HALF)
-        quantise_zm(0, 1)
-        cast_zm(1, 1)
-        quantise_zm(1, 1)
         for b in two:
-            for g in two:
-                gradient(b, g, False)
-        gather(3)
-        weave_atoms(3)
-        weigh_target(1, 1)
+            half_out(b, 0)
         for g in two:
-            residual(2, g)
-        quantise_atoms(3)
-        drain(0, 1)
-        for g in two:
-            interleave(2, g)
-            rebuild(3, g)
-        scatter(0, 1)
-        for g in two:
-            quantise_error(2, g)
-            gradient(2, g, False)
-        for g in two:
-            residual(3, g)
-        drain(1, 1)
-        for g in two:
-            interleave(3, g)
-        scatter(1, 1)
-        for g in two:
-            quantise_error(3, g)
-            gradient(3, g, False)
-        for b in (2, 3):
-            finish(b)
+            cast_zm(g, 1)
+            quantise_zm(g, 1)
+        atoms_ready(3)
+        for b in two:
+            half_out(b, 1)
+        for b, g in ((2, 0), (2, 1), (3, 1), (3, 0)):
+            for step in (rebuild, subtract, weigh, quantise_error):
+                step(b, g)
+        for h in two:
+            half_out(2, h)
+        gradient(LAST, LAST, slice(0, N), 4)
+        nc.vector.tensor_copy(grad_last[:], banks["acc", LAST][:])
+        nc.vector.tensor_copy(result[LAST][:].indirect(offsets[:]), grad_last[:])
+        store(LAST)

@@ -27,8 +27,9 @@ PAIR = 2 * P
 LAST = BLOCKS - 1
 
 GUESTS = {
-    "grad0_0": ("table2", 0),
-    "grad1_0": ("table2", 1024),
+    "atom_codes1": ("diff0_0", 0),
+    "zm_codes0_1": ("table2", 0),
+    "atoms_bf3": ("target_late2_0", 0),
 }
 
 
@@ -69,20 +70,22 @@ def tile_attend_gdi_w_kernel(tc, zT, wT, xm, wt, zm, offs, out):
         doubled = keep.tile([P, PASSES, PACK, 2], F32, name="doubled")
         table = tiles("table", four, [P, T], F32, 4)
         result = tiles("result", four, [P, T], F32, 4)
-        zt_raw = tiles("zt_raw", two, [P, PACK, K_PASS], F32, 4)
+        zt_raw = tile("zt_raw", [P, PACK, R], F32, 4)
         zt_bf = grid("zt_bf", two, two, [P, 2, P, PACK], BF16, 2)
-        zt_codes = grid("zt_codes", two, two, [P, PAIR], U32, 4)
         zt_scales = grid("zt_scales", two, two, [P, PAIR], U8, 1)
-        target = grid("target", two, two, [P, PACK, PAIR], F32, 4)
-        zm_raw = grid("zm_raw", two, two, [P, PACK, HALF], F32, 4)
+        target = tiles("target", two, [P, PACK, PAIR], F32, 4)
+        target_late = grid("target_late", (2, 3), two, [P, PACK, P], F32, 4)
+        zt_codes = grid("zt_codes", two, two, [P, PAIR], U32, 4)
+        zm_first = tile("zm_first", [P, PACK, N], F32, 4)
+        zm_late = tiles("zm_late", two, [P, PACK, HALF], F32, 4)
         zm_bf = grid("zm_bf", two, two, [P, HALF, PACK], BF16, 2)
-        zm_codes = tiles("zm_codes", two, [P, N], U32, 4)
-        zm_scales = tiles("zm_scales", two, [P, N], U8, 1)
+        diff = grid("diff", four, two, [P, PACK, P], F32, 4)
         atoms = tiles("atoms", four, [P, N], BF16, 2)
         atoms_bf = tiles("atoms_bf", four, [P, P * PACK], BF16, 2)
         atom_codes = tiles("atom_codes", four, [P, P], U32, 4)
         atom_scales = tiles("atom_scales", four, [P, P], U8, 1)
-        diff = grid("diff", four, two, [P, PACK, P], F32, 4)
+        zm_codes = grid("zm_codes", two, two, [P, HALF], U32, 4)
+        zm_scales = grid("zm_scales", two, two, [P, HALF], U8, 1)
         err_bf = grid("err_bf", four, two, [P, P, PACK], BF16, 2)
         err_codes = grid("err_codes", four, two, [P, P], U32, 4)
         err_scales = grid("err_scales", four, two, [P, P], U8, 1)
@@ -93,32 +96,30 @@ def tile_attend_gdi_w_kernel(tc, zT, wT, xm, wt, zm, offs, out):
         def load_table(b):
             nc.sync.dma_start(out=table[b][:], in_=wT[b * P:(b + 1) * P, :])
 
-        def load_target(pair, g):
-            rows = xm[0, g * K_PASS:(g + 1) * K_PASS, pair * PAIR:(pair + 1) * PAIR]
-            nc.sync.dma_start(out=target[pair][g][:], in_=rows.rearrange("(p t) d -> p t d", t=PACK))
+        def load_target(dst, g, cols):
+            rows = xm[0, g * K_PASS:(g + 1) * K_PASS, cols]
+            nc.sync.dma_start(out=dst[:], in_=rows.rearrange("(p t) d -> p t d", t=PACK))
 
-        def load_zm(g, h):
-            rows = zm[0, g * K_PASS:(g + 1) * K_PASS, h * HALF:(h + 1) * HALF]
-            nc.sync.dma_start(out=zm_raw[g][h][:], in_=rows.rearrange("(p t) i -> p t i", t=PACK))
+        def load_zm(dst, g, cols):
+            rows = zm[0, g * K_PASS:(g + 1) * K_PASS, cols]
+            nc.sync.dma_start(out=dst[:], in_=rows.rearrange("(p t) i -> p t i", t=PACK))
 
         load_table(0)
         nc.sync.dma_start(offsets[:], offs)
         nc.scalar.dma_start(out=weights[:].rearrange("p (g t) -> p g t", t=PACK),
                             in_=wt[0].rearrange("(g p t) o -> p g (t o)", p=P, t=PACK))
+        nc.sync.dma_start(out=zt_raw[:], in_=zT[0].rearrange("(p j) r -> p j r", j=PACK))
         load_table(1)
         for g in two:
-            nc.sync.dma_start(out=zt_raw[g][:],
-                              in_=zT[0, :, g * K_PASS:(g + 1) * K_PASS].rearrange("(p j) r -> p j r", j=PACK))
-        for g in two:
-            load_target(0, g)
-        for g in two:
-            load_zm(g, 0)
+            load_target(target[g], g, slice(0, PAIR))
+        load_zm(zm_late[0], 1, slice(0, HALF))
+        load_zm(zm_first, 0, slice(0, N))
         load_table(2)
-        for g in two:
-            load_zm(g, 1)
+        load_zm(zm_late[1], 1, slice(HALF, N))
         load_table(3)
-        for g in two:
-            load_target(1, g)
+        for b in (2, 3):
+            for g in two:
+                load_target(target_late[b][g], g, slice(b * P, (b + 1) * P))
 
         make_identity(nc, identity[:])
         nc.gpsimd.memset(result[LAST][:], 0.0)
@@ -130,7 +131,7 @@ def tile_attend_gdi_w_kernel(tc, zT, wT, xm, wt, zm, offs, out):
 
         def gather(b):
             picked = table[b][:].indirect(offsets[:])
-            if b < LAST:
+            if b < 2:
                 nc.scalar.activation(atoms[b][:], picked, COPY)
             else:
                 nc.vector.tensor_copy(atoms[b][:], picked)
@@ -148,7 +149,7 @@ def tile_attend_gdi_w_kernel(tc, zT, wT, xm, wt, zm, offs, out):
             nc.vector.quantize_mx(out=atom_codes[b][:].bitcast(E4M3), scales=atom_scales[b][:], in_=atoms_bf[b][:])
 
         def rebuild(b, g):
-            rec = bank("rec%d_%d" % (b, g), 2 if (b, g) == (LAST, 0) else (b % 2) + 2 * g, [P, PACK, P])
+            rec = bank("rec%d_%d" % (b, g), (b % 2) + 2 * g, [P, PACK, P])
             banks["rec", b, g] = rec
             for t in range(PACK):
                 cols = slice((t % 2) * P, (t % 2 + 1) * P)
@@ -159,7 +160,7 @@ def tile_attend_gdi_w_kernel(tc, zT, wT, xm, wt, zm, offs, out):
                                     start=True, stop=True)
 
         def cast_zt(g, s):
-            src = zt_raw[g][:].rearrange("p j (m t) -> p m j t", t=PACK)[:, :, :, 2 * s:2 * s + 2]
+            src = zt_raw[:, :, g * K_PASS:(g + 1) * K_PASS].rearrange("p j (m t) -> p m j t", t=PACK)[:, :, :, 2 * s:2 * s + 2]
             copy = nc.vector.tensor_copy if s == 0 else nc.scalar.copy
             copy(out=zt_bf[g][s][:].rearrange("p t m j -> p m j t"), in_=src)
 
@@ -168,19 +169,19 @@ def tile_attend_gdi_w_kernel(tc, zT, wT, xm, wt, zm, offs, out):
                                   in_=zt_bf[g][s][:].rearrange("p t m j -> p (t m j)"))
 
         def cast_zm(g, h):
-            src = zm_raw[g][h][:].rearrange("p t (c i) -> p c t i", i=PACK)
+            raw = zm_first[:, :, h * HALF:(h + 1) * HALF] if g == 0 else zm_late[h][:]
+            src = raw.rearrange("p t (c i) -> p c t i", i=PACK)
             dst = zm_bf[g][h][:].rearrange("p (c i) t -> p c t i", i=PACK)
-            copy = nc.scalar.copy if h == 0 else nc.vector.tensor_copy
+            copy = nc.vector.tensor_copy if (g, h) == (1, 1) else nc.scalar.copy
             copy(out=dst, in_=src)
 
         def quantise_zm(g, h):
-            cols = slice(h * HALF, (h + 1) * HALF)
-            nc.vector.quantize_mx(out=zm_codes[g][:, cols].bitcast(E4M3), scales=zm_scales[g][:, cols],
+            nc.vector.quantize_mx(out=zm_codes[g][h][:].bitcast(E4M3), scales=zm_scales[g][h][:],
                                   in_=zm_bf[g][h][:].rearrange("p i t -> p (i t)"))
 
         def subtract(b, g):
-            cols = slice((b % 2) * P, (b % 2 + 1) * P)
-            nc.vector.tensor_tensor(diff[b][g][:], banks["rec", b, g][:], target[b // 2][g][:, :, cols], SUB)
+            rows = target[g][:, :, b * P:(b + 1) * P] if b < 2 else target_late[b][g][:]
+            nc.vector.tensor_tensor(diff[b][g][:], banks["rec", b, g][:], rows, SUB)
 
         def weigh(b, g):
             factor = doubled[:, g:g + 1, :, :]
@@ -192,15 +193,14 @@ def tile_attend_gdi_w_kernel(tc, zT, wT, xm, wt, zm, offs, out):
             nc.vector.quantize_mx(out=err_codes[b][g][:].bitcast(E5M2), scales=err_scales[b][g][:],
                                   in_=err_bf[b][g][:].rearrange("p d t -> p (d t)"))
 
-        def gradient(key, b, cols, number):
-            acc = bank("acc%d_%d" % (b, cols.start), number, [P, cols.stop - cols.start])
-            banks["acc", key] = acc
-            order = (1, 0) if b == LAST else (0, 1)
-            for g in order:
+        def gradient(b, h, number):
+            acc = bank("acc%d_%d" % (b, h), number, [P, HALF])
+            banks["acc", b, h] = acc
+            for g in two:
                 nc.tensor.matmul_mx(out=acc[:],
                                     lhsT=err_codes[b][g][:].bitcast(E5M2), lhsT_scale=err_scales[b][g][:],
-                                    rhs=zm_codes[g][:, cols].bitcast(E4M3), rhs_scale=zm_scales[g][:, cols],
-                                    start=(g == order[0]), stop=(g == order[1]))
+                                    rhs=zm_codes[g][h][:].bitcast(E4M3), rhs_scale=zm_scales[g][h][:],
+                                    start=(g == 0), stop=(g == PASSES - 1))
 
         def store(b):
             if b < LAST:
@@ -209,9 +209,11 @@ def tile_attend_gdi_w_kernel(tc, zT, wT, xm, wt, zm, offs, out):
                 for queue, cols in ((nc.sync, slice(0, T // 2)), (nc.scalar, slice(T // 2, T))):
                     queue.dma_start(out=out[b * P:(b + 1) * P, cols], in_=result[b][:, cols])
 
-        def half_out(b, h):
-            gradient((b, h), b, slice(h * HALF, (h + 1) * HALF), 6 + (b + h) % 2)
-            nc.scalar.copy(out=grad[b][h][:], in_=banks["acc", (b, h)][:])
+        def drain(b, h):
+            gradient(b, h, 6 + (b if b < 2 else h))
+            nc.scalar.copy(out=grad[b][h][:], in_=banks["acc", b, h][:])
+
+        def scatter(b, h):
             nc.scalar.activation(result[b][:].indirect(offsets[:, h * HALF // 16:(h + 1) * HALF // 16]),
                                  grad[b][h][:], COPY)
             if h == 1:
@@ -222,37 +224,55 @@ def tile_attend_gdi_w_kernel(tc, zT, wT, xm, wt, zm, offs, out):
             weave_atoms(b)
             quantise_atoms(b)
 
-        def errors(pair, g):
-            blocks = (2 * pair, 2 * pair + 1)
+        def error(b, g):
             for step in (rebuild, subtract, weigh, quantise_error):
-                for b in blocks:
-                    step(b, g)
+                step(b, g)
 
-        for b in two:
-            atoms_ready(b)
+        def send_half(h):
+            for step in (drain, scatter):
+                for b in two:
+                    step(b, h)
+
+        def zm_ready(g, h):
+            cast_zm(g, h)
+            quantise_zm(g, h)
+
+        atoms_ready(0)
         for g in two:
             for step in (cast_zt, quantise_zt):
                 for s in two:
                     step(g, s)
-        for g in two:
-            errors(0, g)
-            cast_zm(g, 0)
-            quantise_zm(g, 0)
-        atoms_ready(2)
-        for b in two:
-            half_out(b, 0)
-        for g in two:
-            cast_zm(g, 1)
-            quantise_zm(g, 1)
-        atoms_ready(3)
-        for b in two:
-            half_out(b, 1)
-        for b, g in ((2, 0), (2, 1), (3, 1), (3, 0)):
-            for step in (rebuild, subtract, weigh, quantise_error):
-                step(b, g)
+        error(0, 0)
+        atoms_ready(1)
+        error(0, 1)
+        error(1, 0)
+        error(1, 1)
+        for g in (1, 0):
+            zm_ready(g, 0)
+        cast_zm(0, 1)
+        send_half(0)
+        gather(2)
+        quantise_zm(0, 1)
+        cast_zm(1, 1)
+        weave_atoms(2)
+        quantise_zm(1, 1)
+        quantise_atoms(2)
+        gather(3)
+        send_half(1)
+        rebuild(2, 0)
+        subtract(2, 0)
+        weave_atoms(3)
+        weigh(2, 0)
+        quantise_atoms(3)
+        quantise_error(2, 0)
+        for b, g in ((2, 1), (3, 0), (3, 1)):
+            error(b, g)
+        for step in (drain, scatter):
+            for h in two:
+                step(2, h)
         for h in two:
-            half_out(2, h)
-        gradient(LAST, LAST, slice(0, N), 4)
-        nc.vector.tensor_copy(grad_last[:], banks["acc", LAST][:])
+            gradient(LAST, h, 4 + h)
+        for h in two:
+            nc.vector.tensor_copy(grad_last[:, h * HALF:(h + 1) * HALF], banks["acc", LAST, h][:])
         nc.vector.tensor_copy(result[LAST][:].indirect(offsets[:]), grad_last[:])
         store(LAST)

@@ -27,6 +27,7 @@ PAIR = 2 * P
 LAST = BLOCKS - 1
 
 GUESTS = {
+    "atoms_bf2": ("zm_late1", 0),
     "atom_codes1": ("diff0_0", 0),
     "zm_codes0_1": ("table2", 0),
     "atoms_bf3": ("target_late2_0", 0),

from contextlib import ExitStack

import concourse.mybir as mybir
from concourse.masks import make_identity

N, T, D, R = 512, 2048, 512, 1024
FLOPS = 2 * 2 * N * D * R

F32 = mybir.dt.float32
BF16 = mybir.dt.bfloat16
U32 = mybir.dt.uint32
U16 = mybir.dt.uint16
U8 = mybir.dt.uint8
E4M3 = mybir.dt.float8_e4m3fn_x4
E5M2 = mybir.dt.float8_e5m2_x4
COPY = mybir.ActivationFunctionType.Copy
MULT = mybir.AluOpType.mult
SUB = mybir.AluOpType.subtract

P = 128
PACK = 4
K_PASS = P * PACK
BLOCKS = D // P
PASSES = R // K_PASS
HALF = N // 2
PAIR = 2 * P
LAST = BLOCKS - 1

GUESTS = {
    "atoms_bf2": ("zm_late1", 0),
    "atom_codes1": ("diff0_0", 0),
    "zm_codes0_1": ("table2", 0),
    "atoms_bf3": ("target_late2_0", 0),
}


def tile_attend_gdi_w_kernel(tc, zT, wT, xm, wt, zm, offs, out):
    nc = tc.nc
    with ExitStack() as ctx:
        keep = ctx.enter_context(tc.tile_pool(name="keep", bufs=1))
        shared = ctx.enter_context(tc.tile_pool(name="shared", bufs=1))
        psum = ctx.enter_context(tc.psum_pool(name="psum", bufs=1))
        places = {"end": 0}

        def tile(name, shape, dtype, item):
            if name in GUESTS:
                host, first = GUESTS[name]
                places[name] = places[host] + first
            else:
                size = item
                for count in shape[1:]:
                    size = size * count
                places[name] = places["end"]
                places["end"] = places["end"] + size
            return shared.tile(shape, dtype, name=name, align_bytes=64, offset=places[name])

        def tiles(name, keys, shape, dtype, item):
            return {k: tile("%s%d" % (name, k), shape, dtype, item) for k in keys}

        def grid(name, rows, keys, shape, dtype, item):
            return {a: tiles("%s%d_" % (name, a), keys, shape, dtype, item) for a in rows}

        def bank(name, number, shape):
            return psum.tile(shape, F32, name=name, tag="bank%d" % number)

        two = range(2)
        four = range(BLOCKS)
        offsets = keep.tile([P, N // 16], U16, name="offsets")
        weights = keep.tile([P, PASSES * PACK], F32, name="weights")
        identity = keep.tile([P, P], F32, name="identity")
        doubled = keep.tile([P, PASSES, PACK, 2], F32, name="doubled")
        table = tiles("table", four, [P, T], F32, 4)
        result = tiles("result", four, [P, T], F32, 4)
        zt_raw = tile("zt_raw", [P, PACK, R], F32, 4)
        zt_bf = grid("zt_bf", two, two, [P, 2, P, PACK], BF16, 2)
        zt_scales = grid("zt_scales", two, two, [P, PAIR], U8, 1)
        target = tiles("target", two, [P, PACK, PAIR], F32, 4)
        target_late = grid("target_late", (2, 3), two, [P, PACK, P], F32, 4)
        zt_codes = grid("zt_codes", two, two, [P, PAIR], U32, 4)
        zm_first = tile("zm_first", [P, PACK, N], F32, 4)
        zm_late = tiles("zm_late", two, [P, PACK, HALF], F32, 4)
        zm_bf = grid("zm_bf", two, two, [P, HALF, PACK], BF16, 2)
        diff = grid("diff", four, two, [P, PACK, P], F32, 4)
        atoms = tiles("atoms", four, [P, N], BF16, 2)
        atoms_bf = tiles("atoms_bf", four, [P, P * PACK], BF16, 2)
        atom_codes = tiles("atom_codes", four, [P, P], U32, 4)
        atom_scales = tiles("atom_scales", four, [P, P], U8, 1)
        zm_codes = grid("zm_codes", two, two, [P, HALF], U32, 4)
        zm_scales = grid("zm_scales", two, two, [P, HALF], U8, 1)
        err_bf = grid("err_bf", four, two, [P, P, PACK], BF16, 2)
        err_codes = grid("err_codes", four, two, [P, P], U32, 4)
        err_scales = grid("err_scales", four, two, [P, P], U8, 1)
        grad = grid("grad", four, two, [P, HALF], F32, 4)
        grad_last = tile("grad_last", [P, N], F32, 4)
        banks = {}

        def load_table(b):
            nc.sync.dma_start(out=table[b][:], in_=wT[b * P:(b + 1) * P, :])

        def load_target(dst, g, cols):
            rows = xm[0, g * K_PASS:(g + 1) * K_PASS, cols]
            nc.sync.dma_start(out=dst[:], in_=rows.rearrange("(p t) d -> p t d", t=PACK))

        def load_zm(dst, g, cols):
            rows = zm[0, g * K_PASS:(g + 1) * K_PASS, cols]
            nc.sync.dma_start(out=dst[:], in_=rows.rearrange("(p t) i -> p t i", t=PACK))

        load_table(0)
        nc.sync.dma_start(offsets[:], offs)
        nc.scalar.dma_start(out=weights[:].rearrange("p (g t) -> p g t", t=PACK),
                            in_=wt[0].rearrange("(g p t) o -> p g (t o)", p=P, t=PACK))
        nc.sync.dma_start(out=zt_raw[:], in_=zT[0].rearrange("(p j) r -> p j r", j=PACK))
        load_table(1)
        for g in two:
            load_target(target[g], g, slice(0, PAIR))
        load_zm(zm_late[0], 1, slice(0, HALF))
        load_zm(zm_first, 0, slice(0, N))
        load_table(2)
        load_zm(zm_late[1], 1, slice(HALF, N))
        load_table(3)
        for b in (2, 3):
            for g in two:
                load_target(target_late[b][g], g, slice(b * P, (b + 1) * P))

        make_identity(nc, identity[:])
        nc.gpsimd.memset(result[LAST][:], 0.0)
        for b in range(LAST):
            nc.vector.memset(result[b][:], 0.0)

        nc.scalar.copy(out=doubled[:], in_=weights[:].rearrange("p (g t i) -> p g t i", g=PASSES, i=1)
                       .to_broadcast([P, PASSES, PACK, 2]))

        def gather(b):
            picked = table[b][:].indirect(offsets[:])
            if b < 2:
                nc.scalar.activation(atoms[b][:], picked, COPY)
            else:
                nc.vector.tensor_copy(atoms[b][:], picked)
            words = atoms[b][:].bitcast(F32)
            banks["turned", b] = bank("turned%d" % b, 4 + b % 2, [P, 2, P])
            for u in two:
                nc.tensor.transpose(banks["turned", b][:, u, :], words[:, u:HALF:2], identity[:])

        def weave_atoms(b):
            copy = nc.scalar.copy if b < 2 else nc.vector.tensor_copy
            copy(out=atoms_bf[b][:].bitcast(F32).rearrange("p (d u) -> p d u", u=2),
                 in_=banks["turned", b][:].rearrange("p u d -> p d u"))

        def quantise_atoms(b):
            nc.vector.quantize_mx(out=atom_codes[b][:].bitcast(E4M3), scales=atom_scales[b][:], in_=atoms_bf[b][:])

        def rebuild(b, g):
            rec = bank("rec%d_%d" % (b, g), (b % 2) + 2 * g, [P, PACK, P])
            banks["rec", b, g] = rec
            for t in range(PACK):
                cols = slice((t % 2) * P, (t % 2 + 1) * P)
                nc.tensor.matmul_mx(out=rec[:, t, :],
                                    lhsT=zt_codes[g][t // 2][:, cols].bitcast(E4M3),
                                    lhsT_scale=zt_scales[g][t // 2][:, cols],
                                    rhs=atom_codes[b][:].bitcast(E4M3), rhs_scale=atom_scales[b][:],
                                    start=True, stop=True)

        def cast_zt(g, s):
            src = zt_raw[:, :, g * K_PASS:(g + 1) * K_PASS].rearrange("p j (m t) -> p m j t", t=PACK)[:, :, :, 2 * s:2 * s + 2]
            copy = nc.vector.tensor_copy if s == 0 else nc.scalar.copy
            copy(out=zt_bf[g][s][:].rearrange("p t m j -> p m j t"), in_=src)

        def quantise_zt(g, s):
            nc.vector.quantize_mx(out=zt_codes[g][s][:].bitcast(E4M3), scales=zt_scales[g][s][:],
                                  in_=zt_bf[g][s][:].rearrange("p t m j -> p (t m j)"))

        def cast_zm(g, h):
            raw = zm_first[:, :, h * HALF:(h + 1) * HALF] if g == 0 else zm_late[h][:]
            src = raw.rearrange("p t (c i) -> p c t i", i=PACK)
            dst = zm_bf[g][h][:].rearrange("p (c i) t -> p c t i", i=PACK)
            copy = nc.vector.tensor_copy if (g, h) == (1, 1) else nc.scalar.copy
            copy(out=dst, in_=src)

        def quantise_zm(g, h):
            nc.vector.quantize_mx(out=zm_codes[g][h][:].bitcast(E4M3), scales=zm_scales[g][h][:],
                                  in_=zm_bf[g][h][:].rearrange("p i t -> p (i t)"))

        def subtract(b, g):
            rows = target[g][:, :, b * P:(b + 1) * P] if b < 2 else target_late[b][g][:]
            nc.vector.tensor_tensor(diff[b][g][:], banks["rec", b, g][:], rows, SUB)

        def weigh(b, g):
            factor = doubled[:, g:g + 1, :, :]
            nc.vector.tensor_tensor(err_bf[b][g][:].rearrange("p (c i) t -> p c t i", i=2),
                                    diff[b][g][:].rearrange("p t (c i) -> p c t i", i=2),
                                    factor.to_broadcast([P, P // 2, PACK, 2]), MULT)

        def quantise_error(b, g):
            nc.vector.quantize_mx(out=err_codes[b][g][:].bitcast(E5M2), scales=err_scales[b][g][:],
                                  in_=err_bf[b][g][:].rearrange("p d t -> p (d t)"))

        def gradient(b, h, number):
            acc = bank("acc%d_%d" % (b, h), number, [P, HALF])
            banks["acc", b, h] = acc
            for g in two:
                nc.tensor.matmul_mx(out=acc[:],
                                    lhsT=err_codes[b][g][:].bitcast(E5M2), lhsT_scale=err_scales[b][g][:],
                                    rhs=zm_codes[g][h][:].bitcast(E4M3), rhs_scale=zm_scales[g][h][:],
                                    start=(g == 0), stop=(g == PASSES - 1))

        def store(b):
            if b < LAST:
                nc.sync.dma_start(out=out[b * P:(b + 1) * P, :], in_=result[b][:])
            else:
                for queue, cols in ((nc.sync, slice(0, T // 2)), (nc.scalar, slice(T // 2, T))):
                    queue.dma_start(out=out[b * P:(b + 1) * P, cols], in_=result[b][:, cols])

        def drain(b, h):
            gradient(b, h, 6 + (b if b < 2 else h))
            nc.scalar.copy(out=grad[b][h][:], in_=banks["acc", b, h][:])

        def scatter(b, h):
            nc.scalar.activation(result[b][:].indirect(offsets[:, h * HALF // 16:(h + 1) * HALF // 16]),
                                 grad[b][h][:], COPY)
            if h == 1:
                store(b)

        def atoms_ready(b):
            gather(b)
            weave_atoms(b)
            quantise_atoms(b)

        def error(b, g):
            for step in (rebuild, subtract, weigh, quantise_error):
                step(b, g)

        def send_half(h):
            for step in (drain, scatter):
                for b in two:
                    step(b, h)

        def zm_ready(g, h):
            cast_zm(g, h)
            quantise_zm(g, h)

        atoms_ready(0)
        for g in two:
            for step in (cast_zt, quantise_zt):
                for s in two:
                    step(g, s)
        error(0, 0)
        atoms_ready(1)
        error(0, 1)
        error(1, 0)
        error(1, 1)
        for g in (1, 0):
            zm_ready(g, 0)
        cast_zm(0, 1)
        send_half(0)
        gather(2)
        quantise_zm(0, 1)
        cast_zm(1, 1)
        weave_atoms(2)
        quantise_zm(1, 1)
        quantise_atoms(2)
        gather(3)
        send_half(1)
        rebuild(2, 0)
        subtract(2, 0)
        weave_atoms(3)
        weigh(2, 0)
        quantise_atoms(3)
        quantise_error(2, 0)
        for b, g in ((2, 1), (3, 0), (3, 1)):
            error(b, g)
        for step in (drain, scatter):
            for h in two:
                step(2, h)
        for h in two:
            gradient(LAST, h, 4 + h)
        for h in two:
            nc.vector.tensor_copy(grad_last[:, h * HALF:(h + 1) * HALF], banks["acc", LAST, h][:])
        nc.vector.tensor_copy(result[LAST][:].indirect(offsets[:]), grad_last[:])
        store(LAST)
